import numpy as np
import ml_dtypes


def mxq(x, axis, fmt="e4m3"):
    dtype, down = {"e4m3": (ml_dtypes.float8_e4m3fn, 7), "e5m2": (ml_dtypes.float8_e5m2, 14)}[fmt]
    v = np.moveaxis(np.asarray(x, np.float32).astype(ml_dtypes.bfloat16).astype(np.float64), axis, -1)
    blocks = v.reshape(v.shape[:-1] + (-1, 32))
    amax = np.abs(blocks).max(-1, keepdims=True)
    byte = np.maximum(np.where(amax > 0, np.frexp(amax)[1] - 1 + 127, 0) - down, 1)
    scale = np.exp2(byte - 127.0)
    codes = (blocks / scale).astype(np.float32).astype(dtype).astype(np.float64)
    return np.moveaxis((codes * scale).reshape(v.shape), -1, axis)


WIDE = False


def mx_kscale(k):
    if not WIDE:
        return np.ones(k)
    levels = np.array([10, -10, 5, -5, 0])
    if k % 512:
        return np.exp2(np.random.permutation(np.resize(levels, k // 32))).repeat(32)
    a = np.empty((k // 512, 16))
    for p in range(k // 512):
        a[p, :8] = np.random.permutation(np.resize(levels, 8))
        for g in range(8):
            far = levels[np.abs(levels - a[p, g]) >= 10]
            a[p, g + 8] = far[np.random.randint(len(far))]
    return np.exp2(a.ravel()).repeat(32)


BF16 = ml_dtypes.bfloat16


def bf(x):
    return np.asarray(x, np.float32).astype(BF16)


def f64(x):
    return np.asarray(x).astype(np.float64)


E2M1 = np.array([0.0, 0.5, 1.0, 1.5, 2.0, 3.0, 4.0, 6.0, -0.0, -0.5, -1.0, -1.5, -2.0, -3.0, -4.0, -6.0])


def pack_weight(w, fmt):
    k, n = w.shape
    w = f64(bf(w)).reshape(k // 32, 32, n)
    amax = np.abs(w).max(1)
    if fmt == "e4m3":
        byte = np.frexp(amax)[1] - 1 + 127 - 7
    else:
        mant, ex = np.frexp(amax / 6.0)
        byte = np.where(mant > 0.5, ex, ex - 1) + 127
    byte = np.clip(np.where(amax > 0, byte, 1), 1, 254)
    scaled = (w * np.exp2(127.0 - byte)[:, None, :]).reshape(k, n).astype(np.float32)
    by_word = np.ascontiguousarray(scaled.reshape(k // 512, 128, 4, n).transpose(0, 1, 3, 2))
    if fmt == "e4m3":
        words = by_word.astype(ml_dtypes.float8_e4m3fn).view(np.uint8)
    else:
        c = by_word.astype(ml_dtypes.float4_e2m1fn).view(np.uint8) & 0xF
        words = c[..., 0::2] | (c[..., 1::2] << 4)
    return np.ascontiguousarray(words), np.ascontiguousarray(byte.astype(np.uint8).reshape(k // 512, 16, n))


def unpack_weight(words, scales, fmt):
    g, p, n, _ = words.shape
    if fmt == "e4m3":
        vals = np.ascontiguousarray(words).view(ml_dtypes.float8_e4m3fn).astype(np.float64)
    else:
        nib = np.empty((g, p, n, 4), np.uint8)
        nib[..., 0::2] = words & 0xF
        nib[..., 1::2] = words >> 4
        vals = E2M1[nib]
    vals = vals * np.repeat(np.exp2(scales.astype(np.float64) - 127.0), 8, axis=1)[..., None]
    return vals.transpose(0, 1, 3, 2).reshape(g * 512, n)

def planes(Y):
    n, m = Y.shape
    b = f64(bf(Y)).reshape(n // 32, 32, m)
    amax = np.abs(b).max(1)
    byte = np.clip(np.where(amax > 0, np.frexp(amax)[1] - 1 + 127 - 7, 1), 1, 254)
    codes = (b * np.exp2(127.0 - byte)[:, None, :]).reshape(n, m).astype(np.float32).astype(ml_dtypes.float8_e4m3fn).view(np.uint8)
    words = codes.reshape(n // 512, 128, 4, m).transpose(0, 1, 3, 2)
    return np.ascontiguousarray(words), np.ascontiguousarray(byte.astype(np.uint8).reshape(n // 512, 16, m))


T, D, F = 1024, 1024, 1024

DIV = 32.0


def setup_inputs():
    s, u = mx_kscale(D), mx_kscale(T)
    x = bf(np.random.standard_normal((T, D)) * s)
    y = bf(np.random.standard_normal((T, D)) * s)
    words, scales = pack_weight(np.random.standard_normal((D, F)) / np.sqrt(D) / s[:, None], "e4m3")
    return {"x": x,
            "y": y,
            "w_words": words,
            "w_scales": scales,
            "b": bf(np.random.standard_normal(F) * 0.2 * np.sqrt(DIV / np.sqrt(T))),
            "p": bf((1.0 + 0.1 * np.random.standard_normal(T)) * u),
            "q": bf((1.0 + 0.1 * np.random.standard_normal(T)) / u)}


def weighted_observables(states, wq, b, weights):
    h = (mxq(f64(states), 1, "e4m3") @ wq) + f64(b)[None, :]
    return f64(weights)[:, None] * np.tanh(h)


def core(x, y, w_words, w_scales, b, p, q):
    wq = unpack_weight(w_words, w_scales, "e4m3")
    fx = weighted_observables(x, wq, b, p)
    fy = weighted_observables(y, wq, b, q)
    return (mxq(fx, 0, "e4m3").T @ mxq(fy, 0, "e4m3")) / DIV


def reference(x, y, w_words, w_scales, b, p, q):
    R_out = core(x, y, w_words, w_scales, b, p, q)
    words, scales = planes(R_out.T)
    return R_out, words, scales

@@ -1,0 +1,470 @@
+from contextlib import ExitStack
+
+import concourse.mybir as mybir
+from concourse.masks import make_identity
+
+T = D = F = 1024
+P = 128
+FLOPS = 3 * 2 * 1024 * 1024 * 1024
+
+F32 = mybir.dt.float32
+BF16 = mybir.dt.bfloat16
+U32 = mybir.dt.uint32
+I32 = mybir.dt.int32
+U8 = mybir.dt.uint8
+FP8X4 = mybir.dt.float8_e4m3fn_x4
+ACT = mybir.ActivationFunctionType
+ALU = mybir.AluOpType
+INV_DIV = 1.0 / 32.0
+
+BK = 4
+HB = 4
+WARM = 3
+TURNED = {(4, 0), (5, 0)}
+SOFF = {0, 1}
+BIAS_AT = [-8.5, -1.4, -0.4, 3.5, 6.2]
+TURN_AT = [-1.8, 1.7, 5.3, 5.8, 6.6, 6.8, 7.2, 7.4, 9.3, 11.7, 12.4, 12.5, 13.1, 15.8, 16.8, 17.8]
+COPY_AT = [3.3, 3.8, 5.8, 6.5, 6.7, 7.3, 7.4, 8.4, 11.8, 13.6, 15.5, 15.9, 13.8, 17.1, 18.0, 19.0]
+TURN_QUANT = 0.8
+MM_AT = [[4.1, 4.8, 8.6, 8.8], [9.1, 9.9, 10.7, 11.5], [15.6, 13.5, 14.3, 16.3], [13.6, 13.2, 16.5, 16.0], [18.0, 18.0, 20.7, 20.8], [18.8, 19.4, 20.4, 22.7], [19.0, 23.1, 24.1, 27.5], [26.0, 30.4, 31.7, 33.2]]
+BIAS_START = [[5.2, 5.7, 8.6, 9.0], [10.6, 12.3, 12.7, 12.8], [17.0, 17.3, 17.4, 21.5], [15.6, 16.3, 17.5, 22.9], [20.8, 20.9, 23.0, 23.1], [21.47, 22.12, 23.63, 26.87], [27.4, 30.0, 30.5, 31.8], [32.6, 34.0, 34.9, 35.2]]
+WEIGH_AT = [13.0, 17.51, 27.2, 28.8, 25.7, 27.7, 32.1, 36.4]
+WEIGH_STEP = 1.3
+SW_LAG = 1.7
+Z_TANH = 0.4
+Z_TURN = 1.4
+TANH_LAG = 0.55
+QUANT_LAG = 1.5
+BLOCKS = [[0, [0, 1], 26.6, 0.5], [1, [0, 1], 30.87, 0.54], [1, [2], 36.9, 0.5], [0, [2], 36.3, 0.5], [1, [3], 40.8, 0.5], [0, [3], 46.0, 0.5]]
+OUT_LAG = [0.6, 0.6, 0.6, 0.6, 0.6, 0.6, 0.6, 0.6, 0.6, 0.6, 0.6, 0.6, 0.6, 0.6, 0.6, 0.6, 0.6, 0.6, 0.6, 0.6, 0.6, 0.6, 0.6, 0.6, 0.6, 0.6, 0.6, 0.6, 0.6, 0.6, 0.6, 0.6]
+PLANE_LAG = 2.17
+COPY_BY = 'VSVVSSVSVSSVVSSS'
+OUT_BY = 'SSSSSSSSSSSSSSSVSVSSSSSSSVSSSVSS'
+
+
+def tile_extendeddmdkoopmancrossmoment_x2_kernel(
+    tc, x, y, w_words, w_scales, b, p, q, out_0, out_1, out_2
+):
+    nc = tc.nc
+    with ExitStack() as ctx:
+        keep = ctx.enter_context(tc.tile_pool(name="keep", bufs=1))
+        work = ctx.enter_context(tc.tile_pool(name="work", bufs=3))
+        psum = ctx.enter_context(tc.psum_pool(name="psum", bufs=1))
+        ctx.enter_context(tc.manual_schedule())
+
+        ident = keep.tile([P, P], F32, name="ident", align_bytes=64)
+        make_identity(nc, ident[:])
+        w_sc = keep.tile([P, F], U8, name="w_sc", align_bytes=64)
+        nc.vector.memset(w_sc[:].bitcast(I32), 0)
+        warm = keep.tile([P, 1], F32, name="warm")
+        nc.vector.memset(warm[:], 0.0)
+        warm2 = keep.tile([P, 1], F32, name="warm2")
+        b_col = keep.tile([P, 8], BF16, name="b_col", align_bytes=64)
+        nc.scalar.dma_start(out=b_col[:], in_=b.rearrange("(n w) -> n w", w=8))
+        for quad in range(4):
+            nc.scalar.dma_start(
+                out=w_sc[32 * quad : 32 * quad + 8, :].bitcast(I32),
+                in_=w_scales[:, 4 * quad : 4 * quad + 4, :].bitcast(I32),
+            )
+        nc.scalar.activation(out=warm2[:], in_=warm[:], func=ACT.Tanh)
+
+        rows = {"y": y.rearrange("(g p j) d -> g p j d", g=2, j=4), "x": x.rearrange("(g p j) d -> g p j d", g=2, j=4)}
+        raw = {}
+
+        def load_rows(op, g, j0, n):
+            t = keep.tile([P, n, D], BF16, name=f"raw_{op}{g}{j0}", align_bytes=64)
+            nc.sync.dma_start(out=t[:], in_=rows[op][g, :, j0 : j0 + n, :])
+            for k in range(n):
+                raw[op, g, j0 + k] = t[:, k, :].bitcast(F32)
+
+        w_q = keep.tile([P, 2, F], U32, name="w_q", align_bytes=64)
+        w_src = w_words.rearrange("g p n t -> p g (n t)")
+
+        def load_w(h):
+            nc.sync.dma_start(
+                out=w_q[:, :, 512 * h : 512 * h + 512].bitcast(I32),
+                in_=w_src[:, :, 2048 * h : 2048 * h + 2048].bitcast(I32),
+            )
+
+        wt = {}
+        wt32 = {}
+
+        def load_weights(op, src):
+            t = keep.tile([P, 2, 4], BF16, name=f"wt_{op}", align_bytes=64)
+            nc.sync.dma_start(out=t[:], in_=src.rearrange("(g p j) -> p g j", g=2, j=4))
+            t32 = keep.tile([P, 2, 4], F32, name=f"wt32_{op}", align_bytes=64)
+            nc.gpsimd.tensor_copy(out=t32[:], in_=t[:])
+            wt[op] = t
+            wt32[op] = t32
+
+        load_rows("y", 0, 0, 1)
+        load_rows("y", 0, 1, 1)
+        load_w(0)
+        load_rows("y", 0, 2, 2)
+        load_rows("y", 1, 0, 2)
+        load_rows("y", 1, 2, 2)
+        load_weights("y", q)
+        load_weights("x", p)
+        load_rows("x", 0, 0, 4)
+        load_rows("x", 1, 0, 4)
+        load_w(1)
+
+        GROUPS = [("y", 0), ("y", 1), ("x", 0), ("x", 1)]
+        in_q = {}
+        in_s = {}
+        for key in GROUPS:
+            dims = [P, 4, 2, P] if key[0] == "y" else [P, 2, 4, P]
+            in_q[key] = keep.tile(dims, U32, name=f"inq_{key[0]}{key[1]}", align_bytes=64)
+            in_s[key] = keep.tile(dims, U8, name=f"ins_{key[0]}{key[1]}", align_bytes=64)
+
+        def rows_of(key, c, j):
+            if key[0] == "y":
+                return in_q[key][:, j, c, :].bitcast(FP8X4), in_s[key][:, j, c, :]
+            return in_q[key][:, c, j, :].bitcast(FP8X4), in_s[key][:, c, j, :]
+        st = {}
+
+        def turn(key, j):
+            bank = psum.tile([P, 4, P], F32, name="bk", tag="bk", bufs=BK)
+            src = raw[key[0], key[1], j]
+            for cu in range(4):
+                c, u = divmod(cu, 2)
+                nc.tensor.transpose(bank[:, cu, :], src[:, 256 * c + u : 256 * (c + 1) : 2], ident[:])
+            st["turn", key, j] = bank
+
+        def turn_copy(key, j, eng):
+            if ("g4", key, j // 2) not in st:
+                dims = [P, 2, 2, P, 2]
+                st["g4", key, j // 2] = work.tile(dims, F32, name="g4", tag="g4", bufs=3, align_bytes=64)
+            g4 = st["g4", key, j // 2]
+            dst = g4[:, j % 2] if key[0] == "y" else g4[:, :, j % 2]
+            src = st["turn", key, j][:].rearrange("p (c u) r -> p c r u", u=2)
+            if eng == "S":
+                nc.scalar.copy(out=dst, in_=src)
+            else:
+                nc.vector.tensor_copy(out=dst, in_=src)
+
+        def turn_quant(key, j0, n):
+            g4 = st["g4", key, j0 // 2]
+            if key[0] == "y":
+                parts = [(slice(j0, j0 + n), slice(0, 2), slice(j0 % 2, j0 % 2 + n))]
+            else:
+                parts = [(c, slice(j0, j0 + n), c) for c in range(2)]
+            for a, bb, s in parts:
+                src = g4[:, s]
+                if key[0] == "y":
+                    qq, ss, src = in_q[key][:, a], in_s[key][:, a], src.rearrange("p j c r u -> p (j c r u)")
+                    qq, ss = qq.rearrange("p j c r -> p (j c r)"), ss.rearrange("p j c r -> p (j c r)")
+                else:
+                    qq, ss, src = in_q[key][:, a, bb], in_s[key][:, a, bb], src.rearrange("p j r u -> p (j r u)")
+                    qq, ss = qq.rearrange("p j r -> p (j r)"), ss.rearrange("p j r -> p (j r)")
+                nc.vector.quantize_mx(out=qq.bitcast(FP8X4), scales=ss, in_=src.bitcast(BF16))
+
+        nat = keep.tile([P, P, 4], F32, name="b_nat", align_bytes=64)
+        b_nat = nat[:].rearrange("p n m -> p (n m)").bitcast(BF16)
+        b_flat = keep.tile([P, 4, P], F32, name="b_flat", align_bytes=64)
+        b_cols = keep.tile([P, 4], F32, name="b_cols", align_bytes=64)
+
+        def bias_turn():
+            st["bb"] = psum.tile([P, 4, P], F32, name="bk", tag="bk", bufs=BK)
+            for m in range(4):
+                nc.tensor.transpose(st["bb"][:, m, :], b_col[:].bitcast(F32)[:, m : m + 1].to_broadcast([P, P]), ident[:])
+
+        def bias_nat():
+            nc.scalar.copy(out=nat[:], in_=st["bb"][:].rearrange("p m n -> p n m"))
+
+        def bias_flat():
+            nc.scalar.copy(out=b_flat[:].rearrange("p m n -> p (m n)"), in_=b_nat[:, 0:512])
+
+        def bias_flat_turn():
+            st["bf"] = psum.tile([P, 4, P], F32, name="bk", tag="bk", bufs=BK)
+            for m in range(4):
+                nc.tensor.transpose(st["bf"][:, m, :], b_flat[:, m, :], ident[:])
+
+        def bias_cols():
+            nc.scalar.copy(out=b_cols[:], in_=st["bf"][:, :, 0])
+
+        fq = {}
+        fs = {}
+        for h in range(2):
+            for g in range(2):
+                fq["y", h, g] = keep.tile([P, 4, P], U32, name=f"fyq{h}{g}", align_bytes=64)
+                fs["y", h, g] = keep.tile([P, 4, P], U8, name=f"fys{h}{g}", align_bytes=64)
+        for c in range(4):
+            fq["c", c] = keep.tile([P, 2, 256], U32, name=f"fxq{c}", align_bytes=64)
+            fs["c", c] = keep.tile([P, 2, 256], U8, name=f"fxs{c}", align_bytes=64)
+
+        def fx(g, i0, n):
+            c, o = divmod(i0, 256)
+            return fq["c", c][:, g, o : o + n], fs["c", c][:, g, o : o + n]
+
+        UNITS = [("g", "y", 0, 0), ("g", "y", 0, 1), ("g", "y", 1, 0), ("g", "y", 1, 1), ("c", 0), ("c", 1), ("c", 2), ("c", 3)]
+
+        def product(key, j, col0, n, out):
+            for c in range(2):
+                a, a_s = rows_of(key, c, j)
+                nc.tensor.matmul_mx(
+                    out=out,
+                    lhsT=a,
+                    lhsT_scale=a_s,
+                    rhs=w_q[:, c, col0 : col0 + n].bitcast(FP8X4),
+                    rhs_scale=w_sc[4 * c : P, col0 : col0 + n],
+                    start=(c == 0),
+                    stop=(c == 1),
+                )
+
+        def fresh(u):
+            if ("fg", u) not in st:
+                st["fg", u] = work.tile([P, 512, 4], BF16, name="fg", tag="fg", bufs=3, align_bytes=64)
+
+        def mm(u, k):
+            unit = UNITS[u]
+            bank = psum.tile([P, 512], F32, name="hb", tag="hb", bufs=HB)
+            if unit[0] == "g":
+                product((unit[1], unit[3]), k, 512 * unit[2], 512, bank[:])
+            else:
+                for s in range(2):
+                    g, j = divmod(2 * k + s, 4)
+                    product(("x", g), j, 256 * unit[1], 256, bank[:, 256 * s : 256 * s + 256])
+            st["h", u, k] = bank
+
+        def bias(u, k):
+            unit = UNITS[u]
+            if ("z", u) not in st:
+                st["z", u] = work.tile([P, 2048], F32, name="z", tag="z", bufs=3, align_bytes=64)
+            bank = st["h", u, k]
+            dst = st["z", u][:, 512 * k : 512 * k + 512]
+            if unit[0] == "c":
+                bb = b_nat[:, 256 * unit[1] : 256 * unit[1] + 256].unsqueeze(1).to_broadcast([P, 2, 256])
+                nc.vector.tensor_tensor(
+                    out=dst.rearrange("p (s f) -> p s f", s=2), in0=bank[:].rearrange("p (s f) -> p s f", s=2), in1=bb, op=ALU.add
+                )
+            else:
+                nc.vector.tensor_tensor(
+                    out=dst.rearrange("p (c a) -> p c a", c=4),
+                    in0=bank[:].rearrange("p (a c) -> p c a", c=4),
+                    in1=b_nat[:, 512 * unit[2] : 512 * unit[2] + 512].rearrange("p (a c) -> p c a", c=4),
+                    op=ALU.add,
+                )
+
+        def tanh(u, half):
+            if ("th", u) not in st:
+                st["th", u] = work.tile([P, 2048], F32, name="th", tag="th", bufs=3, align_bytes=64)
+            s = slice(1024 * half, 1024 * half + 1024)
+            nc.scalar.activation(out=st["th", u][:, s], in_=st["z", u][:, s], func=ACT.Tanh)
+
+        def weigh(u, half):
+            fresh(u)
+            unit = UNITS[u]
+            th = st["th", u]
+            if unit[0] == "g":
+                n = 512
+                src = th[:].rearrange("p (j f) -> p j f", j=4)
+                w4 = wt[unit[1]][:, unit[3], :]
+            else:
+                n = 256
+                src = th[:, 1024 * half : 1024 * half + 1024].rearrange("p (j f) -> p j f", j=4)
+                w4 = wt["x"][:, half, :]
+            nc.vector.tensor_tensor(
+                out=st["fg", u][:, n * half : n * half + n, :].rearrange("p (c i) j -> p c j i", i=4),
+                in0=src.rearrange("p j (c i) -> p c j i", i=4),
+                in1=w4.unsqueeze(1).unsqueeze(3).to_broadcast([P, n // 4, 4, 4]),
+                op=ALU.mult,
+            )
+
+        def sw(u, j):
+            unit = UNITS[u]
+            if ("gb", u) not in st:
+                st["gb", u] = work.tile([P, 4, 512], BF16, name="gb", tag="gb", bufs=2, align_bytes=64)
+            nc.scalar.activation(
+                out=st["gb", u][:, j, :], in_=st["th", u][:, 512 * j : 512 * j + 512], func=ACT.Copy,
+                scale=wt32[unit[1]][:, unit[3], j : j + 1]
+            )
+
+        def il(u):
+            fresh(u)
+            nc.vector.tensor_copy(
+                out=st["fg", u][:].rearrange("p (c i) j -> p c j i", i=4),
+                in_=st["gb", u][:].rearrange("p j (c i) -> p c j i", i=4),
+            )
+
+        def quant(u):
+            unit = UNITS[u]
+            if unit[0] == "g":
+                key = (unit[1], unit[2], unit[3])
+            else:
+                key = unit
+            nc.vector.quantize_mx(
+                out=fq[key][:].rearrange("p a b -> p (a b)").bitcast(FP8X4),
+                scales=fs[key][:].rearrange("p a b -> p (a b)"),
+                in_=st["fg", u][:].rearrange("p f j -> p (f j)"),
+            )
+
+        def zmm(u, g, ft):
+            c = UNITS[u][1]
+            col0 = 256 * c + 128 * ft
+            bank = psum.tile([P, 512], F32, name="hb", tag="hb", bufs=HB)
+            for ps in range(2):
+                nc.tensor.matmul_mx(
+                    out=bank[:],
+                    lhsT=w_q[:, ps, col0 : col0 + 128].bitcast(FP8X4),
+                    lhsT_scale=w_sc[4 * ps : P, col0 : col0 + 128],
+                    rhs=in_q["x", g][:, ps].rearrange("p j r -> p (j r)").bitcast(FP8X4),
+                    rhs_scale=in_s["x", g][:, ps].rearrange("p j r -> p (j r)"),
+                    start=(ps == 0),
+                    stop=(ps == 1),
+                )
+            st["zh", u, g, ft] = bank
+
+        def ztanh(u, g, ft):
+            c = UNITS[u][1]
+            zt = work.tile([P, 4, P], F32, name="zt", tag="zt", bufs=3, align_bytes=64)
+            nc.scalar.activation(
+                out=zt[:].rearrange("p j r -> p (j r)"), in_=st["zh", u, g, ft][:], func=ACT.Tanh,
+                bias=b_cols[:, 2 * c + ft : 2 * c + ft + 1]
+            )
+            st["zt", u, g, ft] = zt
+
+        def zturn(u, g, ft):
+            bank = psum.tile([P, 4, P], F32, name="bk", tag="bk", bufs=BK)
+            for j in range(4):
+                nc.tensor.transpose(bank[:, j, :], st["zt", u, g, ft][:, j, :], ident[:])
+            st["zb", u, g, ft] = bank
+
+        def zweigh(u, g, ft):
+            fresh(u)
+            f0 = 256 * g + 128 * ft
+            nc.vector.tensor_tensor(
+                out=st["fg", u][:, f0 : f0 + 128, :],
+                in0=st["zb", u, g, ft][:].rearrange("p j f -> p f j"),
+                in1=wt["x"][:, g, :].unsqueeze(1).to_broadcast([P, P, 4]),
+                op=ALU.mult,
+            )
+
+        pl_q = [keep.tile([P, F], U32, name=f"plq{h}", align_bytes=64) for h in range(2)]
+        pl_s = keep.tile([P, F], U8, name="pls", align_bytes=64)
+        out1 = out_1.rearrange("g p m t -> g p (m t)")
+
+        def emit(eng, out, in_):
+            if eng == "S":
+                nc.scalar.activation(out=out, in_=in_, func=ACT.Copy, scale=INV_DIV)
+            else:
+                nc.vector.tensor_scalar(out=out, in0=in_, scalar1=INV_DIV, scalar2=None, op0=ALU.mult)
+
+        def r_mm(it, h):
+            bank = psum.tile([P, 512], F32, name="bk", tag="bk", bufs=BK)
+            for g in range(2):
+                a, a_s = fx(g, 128 * it, 128)
+                nc.tensor.matmul_mx(
+                    out=bank[:], lhsT=a.bitcast(FP8X4), lhsT_scale=a_s,
+                    rhs=fq["y", h, g][:].rearrange("p c a -> p (c a)").bitcast(FP8X4),
+                    rhs_scale=fs["y", h, g][:].rearrange("p c a -> p (c a)"),
+                    start=(g == 0), stop=(g == 1),
+                )
+            st["r", it, h] = bank
+
+        def r_out(it, h, eng):
+            ro = work.tile([P, 512], F32, name="ro", tag="ro", bufs=6, align_bytes=64)
+            emit(eng, ro[:].rearrange("p (a c) -> p a c", c=4), st["r", it, h][:].rearrange("p (c a) -> p a c", c=4))
+            nc.sync.dma_start(out=out_0[128 * it : 128 * it + 128, 512 * h : 512 * h + 512], in_=ro[:])
+
+        def t_mm(h, ic):
+            bank = psum.tile([P, 4, P], F32, name="bk", tag="bk", bufs=BK)
+            for t in range(4):
+                for g in range(2):
+                    m, m_s = fx(g, 128 * ic, 128)
+                    nc.tensor.matmul_mx(
+                        out=bank[:, t, :],
+                        lhsT=fq["y", h, g][:, t, :].bitcast(FP8X4), lhsT_scale=fs["y", h, g][:, t, :],
+                        rhs=m.bitcast(FP8X4), rhs_scale=m_s,
+                        start=(g == 0), stop=(g == 1),
+                    )
+            st["t", h, ic] = bank
+
+        def t_out(h, ic, eng):
+            if ("rt", h, ic // 2) not in st:
+                st["rt", h, ic // 2] = work.tile([P, 256, 4], BF16, name="rt", tag="rt", bufs=4, align_bytes=64)
+            rt = st["rt", h, ic // 2]
+            o = 128 * (ic % 2)
+            emit(eng, rt[:, o : o + 128, :], st["t", h, ic][:].rearrange("p t i -> p i t"))
+
+        def t_quant(h, c):
+            cols = slice(256 * c, 256 * c + 256)
+            nc.vector.quantize_mx(
+                out=pl_q[h][:, cols].bitcast(FP8X4),
+                scales=pl_s[4 * h : P, cols],
+                in_=st["rt", h, c][:].rearrange("p i t -> p (i t)"),
+            )
+            nc.sync.dma_start(
+                out=out1[h][:, 1024 * c : 1024 * c + 1024].bitcast(I32), in_=pl_q[h][:, cols].bitcast(I32)
+            )
+
+        def store_scales(i0, n):
+            for quad in range(4):
+                nc.sync.dma_start(
+                    out=out_2[:, 4 * quad : 4 * quad + 4, i0 : i0 + n].bitcast(I32),
+                    in_=pl_s[32 * quad : 32 * quad + 8, i0 : i0 + n].bitcast(I32),
+                )
+
+        for n in range(WARM):
+            bank = psum.tile([P, 4, P], F32, name="bk", tag="bk", bufs=BK)
+            for m in range(4):
+                nc.tensor.transpose(bank[:, m, :], ident[:], ident[:])
+        ops = []
+
+        def at(t, f, *args):
+            ops.append((t, len(ops), f, args))
+
+        for i, f in enumerate((bias_turn, bias_nat, bias_flat, bias_flat_turn, bias_cols)):
+            at(BIAS_AT[i], f)
+        for n in range(16):
+            key = GROUPS[n // 4]
+            at(TURN_AT[n], turn, key, n % 4)
+            at(COPY_AT[n], turn_copy, key, n % 4, COPY_BY[n])
+            if n < 2:
+                at(COPY_AT[n] + TURN_QUANT, turn_quant, key, n, 1)
+            elif n % 2 == 1:
+                at(max(COPY_AT[n - 1], COPY_AT[n]) + TURN_QUANT, turn_quant, key, n % 4 - 1, 2)
+        for u in range(8):
+            t, v, w = MM_AT[u], BIAS_START[u], WEIGH_AT[u]
+            if (u, 0) in TURNED:
+                for k in range(4):
+                    g, ft = divmod(k, 2)
+                    at(t[k], zmm, u, g, ft)
+                    at(t[k] + Z_TANH, ztanh, u, g, ft)
+                    at(t[k] + Z_TURN, zturn, u, g, ft)
+                    at(v[k], zweigh, u, g, ft)
+                at(w, quant, u)
+            else:
+                for k in range(4):
+                    at(t[k], mm, u, k)
+                    at(v[k], bias, u, k)
+                for half in range(2):
+                    at(v[2 * half + 1] + TANH_LAG, tanh, u, half)
+                if UNITS[u][0] == "c":
+                    for half in range(2):
+                        at(w + WEIGH_STEP * half, weigh, u, half)
+                    at(w + WEIGH_STEP + QUANT_LAG, quant, u)
+                elif u in SOFF:
+                    for j in range(4):
+                        at(v[2 * (j // 2) + 1] + TANH_LAG + SW_LAG + 0.4 * (j % 2), sw, u, j)
+                    at(w, il, u)
+                    at(w + QUANT_LAG, quant, u)
+                else:
+                    at(w, weigh, u, 0)
+                    at(w + QUANT_LAG, quant, u)
+        n = 0
+        for h, chunks, start, step in BLOCKS:
+            t = start
+            for c in chunks:
+                for it in (2 * c, 2 * c + 1):
+                    for f, g, a, e in ((r_mm, r_out, it, h), (t_mm, t_out, h, it)):
+                        at(t, f, a, e)
+                        at(t + OUT_LAG[n], g, a, e, OUT_BY[n])
+                        t += step
+                        n += 1
+                at(t + PLANE_LAG, t_quant, h, c)
+        done = [o[0] for o in ops if o[1] >= 0 and o[2] == t_quant and o[3][1] < 2]
+        at(max(done) + 0.01, store_scales, 0, 512)
+        at(1000.0, store_scales, 512, 512)
+        for o in sorted(ops, key=lambda o: o[:2]):
+            o[2](*o[3])

@@ -3,9 +3,10 @@ from contextlib import ExitStack
 import concourse.mybir as mybir
 from concourse.masks import make_identity
 
-T = D = F = 1024
+SIZE = 1024
 P = 128
-FLOPS = 3 * 2 * 1024 * 1024 * 1024
+FLOPS = 3 * 2 * SIZE * SIZE * SIZE
+INV_DIV = 1.0 / 32.0
 
 F32 = mybir.dt.float32
 BF16 = mybir.dt.bfloat16
@@ -15,31 +16,41 @@ U8 = mybir.dt.uint8
 FP8X4 = mybir.dt.float8_e4m3fn_x4
 ACT = mybir.ActivationFunctionType
 ALU = mybir.AluOpType
-INV_DIV = 1.0 / 32.0
 
-BK = 4
-HB = 4
-WARM = 3
-TURNED = {(4, 0), (5, 0)}
-SOFF = {0, 1}
-BIAS_AT = [-8.5, -1.4, -0.4, 3.5, 6.2]
-TURN_AT = [-1.8, 1.7, 5.3, 5.8, 6.6, 6.8, 7.2, 7.4, 9.3, 11.7, 12.4, 12.5, 13.1, 15.8, 16.8, 17.8]
-COPY_AT = [3.3, 3.8, 5.8, 6.5, 6.7, 7.3, 7.4, 8.4, 11.8, 13.6, 15.5, 15.9, 13.8, 17.1, 18.0, 19.0]
-TURN_QUANT = 0.8
-MM_AT = [[4.1, 4.8, 8.6, 8.8], [9.1, 9.9, 10.7, 11.5], [15.6, 13.5, 14.3, 16.3], [13.6, 13.2, 16.5, 16.0], [18.0, 18.0, 20.7, 20.8], [18.8, 19.4, 20.4, 22.7], [19.0, 23.1, 24.1, 27.5], [26.0, 30.4, 31.7, 33.2]]
-BIAS_START = [[5.2, 5.7, 8.6, 9.0], [10.6, 12.3, 12.7, 12.8], [17.0, 17.3, 17.4, 21.5], [15.6, 16.3, 17.5, 22.9], [20.8, 20.9, 23.0, 23.1], [21.47, 22.12, 23.63, 26.87], [27.4, 30.0, 30.5, 31.8], [32.6, 34.0, 34.9, 35.2]]
-WEIGH_AT = [13.0, 17.51, 27.2, 28.8, 25.7, 27.7, 32.1, 36.4]
-WEIGH_STEP = 1.3
-SW_LAG = 1.7
-Z_TANH = 0.4
-Z_TURN = 1.4
-TANH_LAG = 0.55
-QUANT_LAG = 1.5
-BLOCKS = [[0, [0, 1], 26.6, 0.5], [1, [0, 1], 30.87, 0.54], [1, [2], 36.9, 0.5], [0, [2], 36.3, 0.5], [1, [3], 40.8, 0.5], [0, [3], 46.0, 0.5]]
-OUT_LAG = [0.6, 0.6, 0.6, 0.6, 0.6, 0.6, 0.6, 0.6, 0.6, 0.6, 0.6, 0.6, 0.6, 0.6, 0.6, 0.6, 0.6, 0.6, 0.6, 0.6, 0.6, 0.6, 0.6, 0.6, 0.6, 0.6, 0.6, 0.6, 0.6, 0.6, 0.6, 0.6]
-PLANE_LAG = 2.17
-COPY_BY = 'VSVVSSVSVSSVVSSS'
-OUT_BY = 'SSSSSSSSSSSSSSSVSVSSSSSSSVSSSVSS'
+SUM_BANKS = 4
+TURN_BANKS = 4
+
+SCORE = """
+turn.y.0.0 turn.y.0.1 lift.y.0.0.S spread_bias encode_y.0.0.1 lift_bias.S lift.y.0.1.V dot_y.0.0.0 add_y.0.0.0
+turn.y.0.3 encode_y.0.1.1 turn.y.0.2 lift.y.0.3.V dot_y.0.0.1 lift.y.0.2.S turn.y.1.0 widen_bias add_y.0.0.1
+turn.y.1.1 encode_y.0.2.2 lift.y.1.0.S turn.y.1.2 lift.y.1.1.S dot_y.0.0.2 lift.y.1.2.V tanh_y.0.0.0 dot_y.0.0.3
+encode_y.1.0.2 turn.y.1.3 add_y.0.0.3 turn.x.0.0 add_y.0.0.2 lift.y.1.3.S dot_y.0.1.0 scale_y.0.0.0 encode_y.1.2.2
+dot_y.0.1.1 tanh_y.0.0.1 add_y.0.1.0 dot_y.0.1.2 add_y.0.1.1 dot_y.0.1.3 scale_y.0.0.2 add_y.0.1.2 dot_y.1.0.3
+scale_y.0.0.3 add_y.0.1.3 dot_y.1.0.2 scale_y.0.0.1 add_y.1.0.3 turn.x.0.1 lift.x.0.0.S weave_y.0.0 turn.x.0.3
+lift.x.0.1.S turn.x.1.2 tanh_y.0.1.1 turn.x.0.2 encode_x.0.0 dot_y.1.0.0 add_y.1.0.2 lift.x.1.2.S dot_y.1.1.2
+encode_fy.0.0 lift.x.0.2.S dot_y.1.1.0 add_y.1.0.0 lift.x.0.3.S dot_y.1.1.3 add_y.1.1.0 tanh_y.0.1.0 dot_y.1.0.1
+add_y.1.1.3 turn.x.1.3 scale_y.0.1.3 encode_x.0.2 dot_y.1.1.1 lift.x.1.3.S add_y.1.0.1 turn_bias scale_y.0.1.0
+encode_x.1.2 dot_x.2.0.0 scale_y.0.1.1 add_y.1.1.1 turn.x.1.0 scale_y.0.1.2 add_y.1.1.2 turn.x.1.1 lift.x.1.0.S
+weave_y.0.1 dot_obs.1.0.1 lift_bias_column lift.x.1.1.S dot_obs.1.0.0 tanh_obs.1.0.1 dot_obs.0.0.0 encode_x.1.0
+tanh_obs.1.0.0 dot_obs.0.0.1 add_x.2.0.0 tanh_y.1.0.1 turn_obs.1.0.0 encode_fy.0.1 dot_x.2.0.1 weigh_obs.1.0.0
+tanh_y.1.0.0 turn_obs.1.0.1 add_x.2.0.1 dot_obs.1.1.0 weigh_obs.1.0.1 tanh_obs.0.0.0 dot_obs.1.1.1 weigh_y.1.0
+tanh_obs.1.1.0 dot_obs.0.1.0 tanh_obs.1.1.1 turn_obs.1.1.0 turn_obs.0.0.0 tanh_obs.0.1.0 dot_obs.0.1.1 tanh_obs.0.0.1
+weigh_obs.0.0.0 dot_x.3.0.0 tanh_y.1.1.1 turn_obs.1.1.1 weigh_obs.1.1.0 turn_obs.0.0.1 weigh_obs.1.1.1 dot_x.2.1.0
+tanh_obs.0.1.1 weigh_obs.0.0.1 turn_obs.0.1.0 tanh_x.2.0 encode_fx.1 turn_obs.0.1.1 dot_x.2.1.1 weigh_obs.0.1.1
+tanh_y.1.1.0 cross_t.0.2 weigh_obs.0.1.0 cross.3.0 add_x.2.1.1 lift_cross_t.0.2.S cross_t.0.3 encode_fx.0
+store_cross.3.0.S dot_x.3.0.1 add_x.2.1.0 lift_cross_t.0.3.S cross.1.0 weigh_y.1.1 tanh_x.2.1 cross_t.0.1 cross_t.0.0
+lift_cross_t.0.1.S cross.2.0 lift_cross_t.0.0.S cross.0.0 encode_fy.1.0 store_cross.2.0.S dot_x.3.1.1 encode_fy.1.1
+store_cross.0.0.S add_x.3.0.1 cross.2.1 store_cross.1.0.S add_x.3.0.0 cross.3.1 store_cross.2.1.S weigh_x.2.1
+cross.0.1 tanh_x.3.0 cross_t.1.0 weigh_x.2.0 dot_x.3.1.0 store_cross.0.1.S cross_t.1.2 lift_cross_t.1.0.S add_x.3.1.0
+cross_t.1.1 lift_cross_t.1.2.S encode_fx.2 cross.1.1 store_cross.3.1.S weigh_x.3.0 cross_t.1.3 lift_cross_t.1.1.S
+cross.4.0 store_cross.1.1.S add_x.3.1.1 cross_t.0.4 store_cross.4.0.S lift_cross_t.1.3.V cross.5.0 tanh_x.3.1
+store_plane.1.0 cross_t.0.5 store_cross.5.0.V cross.4.1 lift_cross_t.0.5.S weigh_x.3.1 cross_t.1.5 lift_cross_t.0.4.S
+cross.5.1 store_cross.4.1.S encode_fx.3 cross_t.1.4 store_cross.5.1.S store_plane.0.0 cross_t.1.6 store_plane.1.1
+lift_cross_t.1.5.S cross.6.0 lift_cross_t.1.6.V lift_cross_t.1.4.S cross.6.1 store_plane.0.2 store_cross.6.0.S
+store_plane.0.1 store_scales.0 cross_t.0.7 store_plane.1.2 store_cross.6.1.S cross_t.1.7 lift_cross_t.0.7.S cross.7.1
+cross.7.0 store_cross.7.1.V cross_t.0.6 store_cross.7.0.S lift_cross_t.1.7.V lift_cross_t.0.6.S store_plane.1.3
+store_plane.0.3 store_scales.1
+"""
 
 
 def tile_extendeddmdkoopmancrossmoment_x2_kernel(
@@ -52,419 +63,415 @@ def tile_extendeddmdkoopmancrossmoment_x2_kernel(
         psum = ctx.enter_context(tc.psum_pool(name="psum", bufs=1))
         ctx.enter_context(tc.manual_schedule())
 
+        made = {}
+
+
         ident = keep.tile([P, P], F32, name="ident", align_bytes=64)
         make_identity(nc, ident[:])
-        w_sc = keep.tile([P, F], U8, name="w_sc", align_bytes=64)
-        nc.vector.memset(w_sc[:].bitcast(I32), 0)
-        warm = keep.tile([P, 1], F32, name="warm")
-        nc.vector.memset(warm[:], 0.0)
-        warm2 = keep.tile([P, 1], F32, name="warm2")
-        b_col = keep.tile([P, 8], BF16, name="b_col", align_bytes=64)
-        nc.scalar.dma_start(out=b_col[:], in_=b.rearrange("(n w) -> n w", w=8))
+
+        w_scale = keep.tile([P, SIZE], U8, name="w_scale", align_bytes=64)
+        nc.vector.memset(w_scale[:].bitcast(I32), 0)
+        zero = keep.tile([P, 1], F32, name="zero")
+        nc.vector.memset(zero[:], 0.0)
+
+        b_rows = keep.tile([P, 8], BF16, name="b_rows", align_bytes=64)
+        nc.scalar.dma_start(out=b_rows[:], in_=b.rearrange("(n w) -> n w", w=8))
         for quad in range(4):
             nc.scalar.dma_start(
-                out=w_sc[32 * quad : 32 * quad + 8, :].bitcast(I32),
+                out=w_scale[32 * quad : 32 * quad + 8, :].bitcast(I32),
                 in_=w_scales[:, 4 * quad : 4 * quad + 4, :].bitcast(I32),
             )
-        nc.scalar.activation(out=warm2[:], in_=warm[:], func=ACT.Tanh)
+        tanh_warm_up = keep.tile([P, 1], F32, name="tanh_warm_up")
+        nc.scalar.activation(out=tanh_warm_up[:], in_=zero[:], func=ACT.Tanh)
 
-        rows = {"y": y.rearrange("(g p j) d -> g p j d", g=2, j=4), "x": x.rearrange("(g p j) d -> g p j d", g=2, j=4)}
-        raw = {}
+        row_words = {}
 
-        def load_rows(op, g, j0, n):
-            t = keep.tile([P, n, D], BF16, name=f"raw_{op}{g}{j0}", align_bytes=64)
-            nc.sync.dma_start(out=t[:], in_=rows[op][g, :, j0 : j0 + n, :])
+        def load_rows(op, source, g, j, n):
+            rows = keep.tile([P, n, SIZE], BF16, name=f"rows_{op}{g}{j}", align_bytes=64)
+            nc.sync.dma_start(
+                out=rows[:], in_=source.rearrange("(g p j) d -> g p j d", g=2, j=4)[g, :, j : j + n, :]
+            )
             for k in range(n):
-                raw[op, g, j0 + k] = t[:, k, :].bitcast(F32)
+                row_words[op, g, j + k] = rows[:, k, :].bitcast(F32)
 
-        w_q = keep.tile([P, 2, F], U32, name="w_q", align_bytes=64)
-        w_src = w_words.rearrange("g p n t -> p g (n t)")
+        w_code = keep.tile([P, 2, SIZE], U32, name="w_code", align_bytes=64)
+        w_source = w_words.rearrange("c p n t -> p c (n t)")
 
         def load_w(h):
             nc.sync.dma_start(
-                out=w_q[:, :, 512 * h : 512 * h + 512].bitcast(I32),
-                in_=w_src[:, :, 2048 * h : 2048 * h + 2048].bitcast(I32),
+                out=w_code[:, :, 512 * h : 512 * h + 512].bitcast(I32),
+                in_=w_source[:, :, 2048 * h : 2048 * h + 2048].bitcast(I32),
             )
 
-        wt = {}
-        wt32 = {}
+        weight = {}
+        weight_f32 = {}
 
-        def load_weights(op, src):
-            t = keep.tile([P, 2, 4], BF16, name=f"wt_{op}", align_bytes=64)
-            nc.sync.dma_start(out=t[:], in_=src.rearrange("(g p j) -> p g j", g=2, j=4))
-            t32 = keep.tile([P, 2, 4], F32, name=f"wt32_{op}", align_bytes=64)
-            nc.gpsimd.tensor_copy(out=t32[:], in_=t[:])
-            wt[op] = t
-            wt32[op] = t32
+        def load_weights(op, source):
+            weight[op] = keep.tile([P, 2, 4], BF16, name=f"weight_{op}", align_bytes=64)
+            nc.sync.dma_start(out=weight[op][:], in_=source.rearrange("(g p j) -> p g j", g=2, j=4))
+            weight_f32[op] = keep.tile([P, 2, 4], F32, name=f"weight_f32_{op}", align_bytes=64)
+            nc.gpsimd.tensor_copy(out=weight_f32[op][:], in_=weight[op][:])
 
-        load_rows("y", 0, 0, 1)
-        load_rows("y", 0, 1, 1)
+        load_rows("y", y, 0, 0, 1)
+        load_rows("y", y, 0, 1, 1)
         load_w(0)
-        load_rows("y", 0, 2, 2)
-        load_rows("y", 1, 0, 2)
-        load_rows("y", 1, 2, 2)
+        load_rows("y", y, 0, 2, 2)
+        load_rows("y", y, 1, 0, 2)
+        load_rows("y", y, 1, 2, 2)
         load_weights("y", q)
         load_weights("x", p)
-        load_rows("x", 0, 0, 4)
-        load_rows("x", 1, 0, 4)
+        load_rows("x", x, 0, 0, 4)
+        load_rows("x", x, 1, 0, 4)
         load_w(1)
 
-        GROUPS = [("y", 0), ("y", 1), ("x", 0), ("x", 1)]
-        in_q = {}
-        in_s = {}
-        for key in GROUPS:
-            dims = [P, 4, 2, P] if key[0] == "y" else [P, 2, 4, P]
-            in_q[key] = keep.tile(dims, U32, name=f"inq_{key[0]}{key[1]}", align_bytes=64)
-            in_s[key] = keep.tile(dims, U8, name=f"ins_{key[0]}{key[1]}", align_bytes=64)
+        def turn_bank():
+            bank = psum.tile([P, 4, P], F32, name="turn_bank", tag="turn_bank", bufs=TURN_BANKS)
+            return bank
 
-        def rows_of(key, c, j):
-            if key[0] == "y":
-                return in_q[key][:, j, c, :].bitcast(FP8X4), in_s[key][:, j, c, :]
-            return in_q[key][:, c, j, :].bitcast(FP8X4), in_s[key][:, c, j, :]
-        st = {}
+        def sum_bank():
+            bank = psum.tile([P, 512], F32, name="sum_bank", tag="sum_bank", bufs=SUM_BANKS)
+            return bank
 
-        def turn(key, j):
-            bank = psum.tile([P, 4, P], F32, name="bk", tag="bk", bufs=BK)
-            src = raw[key[0], key[1], j]
-            for cu in range(4):
-                c, u = divmod(cu, 2)
-                nc.tensor.transpose(bank[:, cu, :], src[:, 256 * c + u : 256 * (c + 1) : 2], ident[:])
-            st["turn", key, j] = bank
-
-        def turn_copy(key, j, eng):
-            if ("g4", key, j // 2) not in st:
-                dims = [P, 2, 2, P, 2]
-                st["g4", key, j // 2] = work.tile(dims, F32, name="g4", tag="g4", bufs=3, align_bytes=64)
-            g4 = st["g4", key, j // 2]
-            dst = g4[:, j % 2] if key[0] == "y" else g4[:, :, j % 2]
-            src = st["turn", key, j][:].rearrange("p (c u) r -> p c r u", u=2)
-            if eng == "S":
-                nc.scalar.copy(out=dst, in_=src)
-            else:
-                nc.vector.tensor_copy(out=dst, in_=src)
-
-        def turn_quant(key, j0, n):
-            g4 = st["g4", key, j0 // 2]
-            if key[0] == "y":
-                parts = [(slice(j0, j0 + n), slice(0, 2), slice(j0 % 2, j0 % 2 + n))]
-            else:
-                parts = [(c, slice(j0, j0 + n), c) for c in range(2)]
-            for a, bb, s in parts:
-                src = g4[:, s]
-                if key[0] == "y":
-                    qq, ss, src = in_q[key][:, a], in_s[key][:, a], src.rearrange("p j c r u -> p (j c r u)")
-                    qq, ss = qq.rearrange("p j c r -> p (j c r)"), ss.rearrange("p j c r -> p (j c r)")
-                else:
-                    qq, ss, src = in_q[key][:, a, bb], in_s[key][:, a, bb], src.rearrange("p j r u -> p (j r u)")
-                    qq, ss = qq.rearrange("p j r -> p (j r)"), ss.rearrange("p j r -> p (j r)")
-                nc.vector.quantize_mx(out=qq.bitcast(FP8X4), scales=ss, in_=src.bitcast(BF16))
-
-        nat = keep.tile([P, P, 4], F32, name="b_nat", align_bytes=64)
-        b_nat = nat[:].rearrange("p n m -> p (n m)").bitcast(BF16)
-        b_flat = keep.tile([P, 4, P], F32, name="b_flat", align_bytes=64)
-        b_cols = keep.tile([P, 4], F32, name="b_cols", align_bytes=64)
-
-        def bias_turn():
-            st["bb"] = psum.tile([P, 4, P], F32, name="bk", tag="bk", bufs=BK)
+        for n in range(3):
+            bank = turn_bank()
             for m in range(4):
-                nc.tensor.transpose(st["bb"][:, m, :], b_col[:].bitcast(F32)[:, m : m + 1].to_broadcast([P, P]), ident[:])
+                nc.tensor.transpose(bank[:, m, :], ident[:], ident[:])
 
-        def bias_nat():
-            nc.scalar.copy(out=nat[:], in_=st["bb"][:].rearrange("p m n -> p n m"))
 
-        def bias_flat():
-            nc.scalar.copy(out=b_flat[:].rearrange("p m n -> p (m n)"), in_=b_nat[:, 0:512])
+        row_dims = {"y": [P, 4, 2, P], "x": [P, 2, 4, P]}
+        row_code = {}
+        row_scale = {}
+        for op in ("y", "x"):
+            for g in range(2):
+                row_code[op, g] = keep.tile(row_dims[op], U32, name=f"row_code_{op}{g}", align_bytes=64)
+                row_scale[op, g] = keep.tile(row_dims[op], U8, name=f"row_scale_{op}{g}", align_bytes=64)
 
-        def bias_flat_turn():
-            st["bf"] = psum.tile([P, 4, P], F32, name="bk", tag="bk", bufs=BK)
+        def stationary_rows(op, g, j, c):
+            if op == "y":
+                return row_code[op, g][:, j, c, :].bitcast(FP8X4), row_scale[op, g][:, j, c, :]
+            return row_code[op, g][:, c, j, :].bitcast(FP8X4), row_scale[op, g][:, c, j, :]
+
+        def copy(engine, out, in_):
+            if engine == "S":
+                nc.scalar.copy(out=out, in_=in_)
+            else:
+                nc.vector.tensor_copy(out=out, in_=in_)
+
+        def turn(op, g, j):
+            bank = turn_bank()
+            words = row_words[op, g, j]
+            for c in range(2):
+                for e in range(2):
+                    nc.tensor.transpose(bank[:, 2 * c + e, :], words[:, 256 * c + e : 256 * (c + 1) : 2], ident[:])
+            made["turn", op, g, j] = bank
+
+        def lift(op, g, j, engine):
+            if ("lift", op, g, j // 2) not in made:
+                pair_dims = [P, 2, 2, P, 2]
+                made["lift", op, g, j // 2] = work.tile(pair_dims, F32, name="pair", tag="pair", align_bytes=64)
+            pair = made["lift", op, g, j // 2]
+            out = pair[:, j % 2] if op == "y" else pair[:, :, j % 2]
+            copy(engine, out, made["turn", op, g, j][:].rearrange("p (c e) r -> p c r e", e=2))
+
+        def encode_y(g, j, n):
+            pair = made["lift", "y", g, j // 2]
+            nc.vector.quantize_mx(
+                out=row_code["y", g][:, j : j + n].rearrange("p j c r -> p (j c r)").bitcast(FP8X4),
+                scales=row_scale["y", g][:, j : j + n].rearrange("p j c r -> p (j c r)"),
+                in_=pair[:, j % 2 : j % 2 + n].rearrange("p j c r e -> p (j c r e)").bitcast(BF16),
+            )
+
+        def encode_x(g, j):
+            for c in range(2):
+                nc.vector.quantize_mx(
+                    out=row_code["x", g][:, c, j : j + 2].rearrange("p j r -> p (j r)").bitcast(FP8X4),
+                    scales=row_scale["x", g][:, c, j : j + 2].rearrange("p j r -> p (j r)"),
+                    in_=made["lift", "x", g, j // 2][:, c].rearrange("p j r e -> p (j r e)").bitcast(BF16),
+                )
+
+
+        bias_words = keep.tile([P, P, 4], F32, name="bias_words", align_bytes=64)
+        bias_row = bias_words[:].rearrange("p n m -> p (n m)").bitcast(BF16)
+        bias_f32 = keep.tile([P, 4, P], F32, name="bias_f32", align_bytes=64)
+        bias_column = keep.tile([P, 4], F32, name="bias_column", align_bytes=64)
+
+        def spread_bias():
+            made["spread_bias"] = turn_bank()
+            words = b_rows[:].bitcast(F32)
             for m in range(4):
-                nc.tensor.transpose(st["bf"][:, m, :], b_flat[:, m, :], ident[:])
+                nc.tensor.transpose(made["spread_bias"][:, m, :], words[:, m : m + 1].to_broadcast([P, P]), ident[:])
 
-        def bias_cols():
-            nc.scalar.copy(out=b_cols[:], in_=st["bf"][:, :, 0])
+        def lift_bias(engine):
+            copy(engine, bias_words[:], made["spread_bias"][:].rearrange("p m n -> p n m"))
 
-        fq = {}
-        fs = {}
+        def widen_bias():
+            nc.scalar.copy(out=bias_f32[:].rearrange("p m n -> p (m n)"), in_=bias_row[:, 0:512])
+
+        def turn_bias():
+            made["turn_bias"] = turn_bank()
+            for m in range(4):
+                nc.tensor.transpose(made["turn_bias"][:, m, :], bias_f32[:, m, :], ident[:])
+
+        def lift_bias_column():
+            nc.scalar.copy(out=bias_column[:], in_=made["turn_bias"][:, :, 0])
+
+
+        fy_code = {}
+        fy_scale = {}
         for h in range(2):
             for g in range(2):
-                fq["y", h, g] = keep.tile([P, 4, P], U32, name=f"fyq{h}{g}", align_bytes=64)
-                fs["y", h, g] = keep.tile([P, 4, P], U8, name=f"fys{h}{g}", align_bytes=64)
+                fy_code[h, g] = keep.tile([P, 4, P], U32, name=f"fy_code{h}{g}", align_bytes=64)
+                fy_scale[h, g] = keep.tile([P, 4, P], U8, name=f"fy_scale{h}{g}", align_bytes=64)
+        fx_code = []
+        fx_scale = []
         for c in range(4):
-            fq["c", c] = keep.tile([P, 2, 256], U32, name=f"fxq{c}", align_bytes=64)
-            fs["c", c] = keep.tile([P, 2, 256], U8, name=f"fxs{c}", align_bytes=64)
+            code = keep.tile([P, 2, 256], U32, name=f"fx_code{c}", align_bytes=64)
+            scale = keep.tile([P, 2, 256], U8, name=f"fx_scale{c}", align_bytes=64)
+            fx_code.append(code)
+            fx_scale.append(scale)
 
-        def fx(g, i0, n):
-            c, o = divmod(i0, 256)
-            return fq["c", c][:, g, o : o + n], fs["c", c][:, g, o : o + n]
+        def work_tile(name, key, dims, dtype, bufs):
+            if (name, key) not in made:
+                made[name, key] = work.tile(dims, dtype, name=name, tag=name, bufs=bufs, align_bytes=64)
+            return made[name, key]
 
-        UNITS = [("g", "y", 0, 0), ("g", "y", 0, 1), ("g", "y", 1, 0), ("g", "y", 1, 1), ("c", 0), ("c", 1), ("c", 2), ("c", 3)]
-
-        def product(key, j, col0, n, out):
+        def project(op, g, j, col, n, out):
             for c in range(2):
-                a, a_s = rows_of(key, c, j)
+                code, scale = stationary_rows(op, g, j, c)
                 nc.tensor.matmul_mx(
                     out=out,
-                    lhsT=a,
-                    lhsT_scale=a_s,
-                    rhs=w_q[:, c, col0 : col0 + n].bitcast(FP8X4),
-                    rhs_scale=w_sc[4 * c : P, col0 : col0 + n],
+                    lhsT=code,
+                    lhsT_scale=scale,
+                    rhs=w_code[:, c, col : col + n].bitcast(FP8X4),
+                    rhs_scale=w_scale[4 * c : P, col : col + n],
                     start=(c == 0),
                     stop=(c == 1),
                 )
 
-        def fresh(u):
-            if ("fg", u) not in st:
-                st["fg", u] = work.tile([P, 512, 4], BF16, name="fg", tag="fg", bufs=3, align_bytes=64)
 
-        def mm(u, k):
-            unit = UNITS[u]
-            bank = psum.tile([P, 512], F32, name="hb", tag="hb", bufs=HB)
-            if unit[0] == "g":
-                product((unit[1], unit[3]), k, 512 * unit[2], 512, bank[:])
-            else:
-                for s in range(2):
-                    g, j = divmod(2 * k + s, 4)
-                    product(("x", g), j, 256 * unit[1], 256, bank[:, 256 * s : 256 * s + 256])
-            st["h", u, k] = bank
+        def dot_y(h, g, j):
+            bank = sum_bank()
+            project("y", g, j, 512 * h, 512, bank[:])
+            made["dot_y", h, g, j] = bank
 
-        def bias(u, k):
-            unit = UNITS[u]
-            if ("z", u) not in st:
-                st["z", u] = work.tile([P, 2048], F32, name="z", tag="z", bufs=3, align_bytes=64)
-            bank = st["h", u, k]
-            dst = st["z", u][:, 512 * k : 512 * k + 512]
-            if unit[0] == "c":
-                bb = b_nat[:, 256 * unit[1] : 256 * unit[1] + 256].unsqueeze(1).to_broadcast([P, 2, 256])
-                nc.vector.tensor_tensor(
-                    out=dst.rearrange("p (s f) -> p s f", s=2), in0=bank[:].rearrange("p (s f) -> p s f", s=2), in1=bb, op=ALU.add
-                )
-            else:
-                nc.vector.tensor_tensor(
-                    out=dst.rearrange("p (c a) -> p c a", c=4),
-                    in0=bank[:].rearrange("p (a c) -> p c a", c=4),
-                    in1=b_nat[:, 512 * unit[2] : 512 * unit[2] + 512].rearrange("p (a c) -> p c a", c=4),
-                    op=ALU.add,
-                )
-
-        def tanh(u, half):
-            if ("th", u) not in st:
-                st["th", u] = work.tile([P, 2048], F32, name="th", tag="th", bufs=3, align_bytes=64)
-            s = slice(1024 * half, 1024 * half + 1024)
-            nc.scalar.activation(out=st["th", u][:, s], in_=st["z", u][:, s], func=ACT.Tanh)
-
-        def weigh(u, half):
-            fresh(u)
-            unit = UNITS[u]
-            th = st["th", u]
-            if unit[0] == "g":
-                n = 512
-                src = th[:].rearrange("p (j f) -> p j f", j=4)
-                w4 = wt[unit[1]][:, unit[3], :]
-            else:
-                n = 256
-                src = th[:, 1024 * half : 1024 * half + 1024].rearrange("p (j f) -> p j f", j=4)
-                w4 = wt["x"][:, half, :]
+        def add_y(h, g, j):
+            z = work_tile("z", ("y", h, g), [P, 2048], F32, 3)
             nc.vector.tensor_tensor(
-                out=st["fg", u][:, n * half : n * half + n, :].rearrange("p (c i) j -> p c j i", i=4),
-                in0=src.rearrange("p j (c i) -> p c j i", i=4),
-                in1=w4.unsqueeze(1).unsqueeze(3).to_broadcast([P, n // 4, 4, 4]),
+                out=z[:, 512 * j : 512 * j + 512].rearrange("p (t a) -> p t a", t=4),
+                in0=made["dot_y", h, g, j][:].rearrange("p (a t) -> p t a", t=4),
+                in1=bias_row[:, 512 * h : 512 * h + 512].rearrange("p (a t) -> p t a", t=4),
+                op=ALU.add,
+            )
+
+        def tanh(key, part):
+            span = slice(1024 * part, 1024 * part + 1024)
+            th = work_tile("th", key, [P, 2048], F32, 3)
+            nc.scalar.activation(out=th[:, span], in_=made["z", key][:, span], func=ACT.Tanh)
+
+        def tanh_y(h, g, part):
+            tanh(("y", h, g), part)
+
+        def weave(f, th, weights, n):
+            nc.vector.tensor_tensor(
+                out=f.rearrange("p (o i) j -> p o j i", i=4),
+                in0=th.rearrange("p j (o i) -> p o j i", i=4),
+                in1=weights.unsqueeze(1).unsqueeze(3).to_broadcast([P, n // 4, 4, 4]),
                 op=ALU.mult,
             )
 
-        def sw(u, j):
-            unit = UNITS[u]
-            if ("gb", u) not in st:
-                st["gb", u] = work.tile([P, 4, 512], BF16, name="gb", tag="gb", bufs=2, align_bytes=64)
+        def weigh_y(h, g):
+            f = work_tile("f", ("y", h, g), [P, 512, 4], BF16, 3)
+            weave(f[:], made["th", ("y", h, g)][:].rearrange("p (j o) -> p j o", j=4), weight["y"][:, g, :], 512)
+
+
+        def scale_y(h, g, j):
+            v = work_tile("v", ("y", h, g), [P, 4, 512], BF16, 2)
             nc.scalar.activation(
-                out=st["gb", u][:, j, :], in_=st["th", u][:, 512 * j : 512 * j + 512], func=ACT.Copy,
-                scale=wt32[unit[1]][:, unit[3], j : j + 1]
+                out=v[:, j, :],
+                in_=made["th", ("y", h, g)][:, 512 * j : 512 * j + 512],
+                func=ACT.Copy,
+                scale=weight_f32["y"][:, g, j : j + 1],
             )
 
-        def il(u):
-            fresh(u)
+        def weave_y(h, g):
+            f = work_tile("f", ("y", h, g), [P, 512, 4], BF16, 3)
             nc.vector.tensor_copy(
-                out=st["fg", u][:].rearrange("p (c i) j -> p c j i", i=4),
-                in_=st["gb", u][:].rearrange("p j (c i) -> p c j i", i=4),
+                out=f[:].rearrange("p (o i) j -> p o j i", i=4),
+                in_=made["v", ("y", h, g)][:].rearrange("p j (o i) -> p o j i", i=4),
             )
 
-        def quant(u):
-            unit = UNITS[u]
-            if unit[0] == "g":
-                key = (unit[1], unit[2], unit[3])
-            else:
-                key = unit
+        def encode_fy(h, g):
             nc.vector.quantize_mx(
-                out=fq[key][:].rearrange("p a b -> p (a b)").bitcast(FP8X4),
-                scales=fs[key][:].rearrange("p a b -> p (a b)"),
-                in_=st["fg", u][:].rearrange("p f j -> p (f j)"),
+                out=fy_code[h, g][:].rearrange("p t a -> p (t a)").bitcast(FP8X4),
+                scales=fy_scale[h, g][:].rearrange("p t a -> p (t a)"),
+                in_=made["f", ("y", h, g)][:].rearrange("p o j -> p (o j)"),
             )
 
-        def zmm(u, g, ft):
-            c = UNITS[u][1]
-            col0 = 256 * c + 128 * ft
-            bank = psum.tile([P, 512], F32, name="hb", tag="hb", bufs=HB)
-            for ps in range(2):
+
+        def dot_x(c, g, i):
+            bank = sum_bank()
+            for k in range(2):
+                project("x", g, 2 * i + k, 256 * c, 256, bank[:, 256 * k : 256 * k + 256])
+            made["dot_x", c, g, i] = bank
+
+        def add_x(c, g, i):
+            z = work_tile("z", ("x", c), [P, 2048], F32, 3)
+            first = 1024 * g + 512 * i
+            nc.vector.tensor_tensor(
+                out=z[:, first : first + 512].rearrange("p (k o) -> p k o", k=2),
+                in0=made["dot_x", c, g, i][:].rearrange("p (k o) -> p k o", k=2),
+                in1=bias_row[:, 256 * c : 256 * c + 256].unsqueeze(1).to_broadcast([P, 2, 256]),
+                op=ALU.add,
+            )
+
+        def tanh_x(c, g):
+            tanh(("x", c), g)
+
+        def weigh_x(c, g):
+            f = work_tile("f", ("x", c), [P, 512, 4], BF16, 3)
+            th = made["th", ("x", c)][:, 1024 * g : 1024 * g + 1024].rearrange("p (j o) -> p j o", j=4)
+            weave(f[:, 256 * g : 256 * g + 256, :], th, weight["x"][:, g, :], 256)
+
+
+        def dot_obs(c, g, i):
+            col = 256 * c + 128 * i
+            bank = sum_bank()
+            for k in range(2):
                 nc.tensor.matmul_mx(
                     out=bank[:],
-                    lhsT=w_q[:, ps, col0 : col0 + 128].bitcast(FP8X4),
-                    lhsT_scale=w_sc[4 * ps : P, col0 : col0 + 128],
-                    rhs=in_q["x", g][:, ps].rearrange("p j r -> p (j r)").bitcast(FP8X4),
-                    rhs_scale=in_s["x", g][:, ps].rearrange("p j r -> p (j r)"),
-                    start=(ps == 0),
-                    stop=(ps == 1),
+                    lhsT=w_code[:, k, col : col + P].bitcast(FP8X4),
+                    lhsT_scale=w_scale[4 * k : P, col : col + P],
+                    rhs=row_code["x", g][:, k].rearrange("p j r -> p (j r)").bitcast(FP8X4),
+                    rhs_scale=row_scale["x", g][:, k].rearrange("p j r -> p (j r)"),
+                    start=(k == 0),
+                    stop=(k == 1),
                 )
-            st["zh", u, g, ft] = bank
+            made["dot_obs", c, g, i] = bank
 
-        def ztanh(u, g, ft):
-            c = UNITS[u][1]
-            zt = work.tile([P, 4, P], F32, name="zt", tag="zt", bufs=3, align_bytes=64)
+        def tanh_obs(c, g, i):
+            t = work_tile("t", (c, g, i), [P, 4, P], F32, 3)
             nc.scalar.activation(
-                out=zt[:].rearrange("p j r -> p (j r)"), in_=st["zh", u, g, ft][:], func=ACT.Tanh,
-                bias=b_cols[:, 2 * c + ft : 2 * c + ft + 1]
+                out=t[:].rearrange("p j r -> p (j r)"),
+                in_=made["dot_obs", c, g, i][:],
+                func=ACT.Tanh,
+                bias=bias_column[:, 2 * c + i : 2 * c + i + 1],
             )
-            st["zt", u, g, ft] = zt
 
-        def zturn(u, g, ft):
-            bank = psum.tile([P, 4, P], F32, name="bk", tag="bk", bufs=BK)
+        def turn_obs(c, g, i):
+            bank = turn_bank()
             for j in range(4):
-                nc.tensor.transpose(bank[:, j, :], st["zt", u, g, ft][:, j, :], ident[:])
-            st["zb", u, g, ft] = bank
+                nc.tensor.transpose(bank[:, j, :], made["t", (c, g, i)][:, j, :], ident[:])
+            made["turn_obs", c, g, i] = bank
 
-        def zweigh(u, g, ft):
-            fresh(u)
-            f0 = 256 * g + 128 * ft
+        def weigh_obs(c, g, i):
+            f = work_tile("f", ("x", c), [P, 512, 4], BF16, 3)
+            first = 256 * g + 128 * i
             nc.vector.tensor_tensor(
-                out=st["fg", u][:, f0 : f0 + 128, :],
-                in0=st["zb", u, g, ft][:].rearrange("p j f -> p f j"),
-                in1=wt["x"][:, g, :].unsqueeze(1).to_broadcast([P, P, 4]),
+                out=f[:, first : first + P, :],
+                in0=made["turn_obs", c, g, i][:].rearrange("p j o -> p o j"),
+                in1=weight["x"][:, g, :].unsqueeze(1).to_broadcast([P, P, 4]),
                 op=ALU.mult,
             )
 
-        pl_q = [keep.tile([P, F], U32, name=f"plq{h}", align_bytes=64) for h in range(2)]
-        pl_s = keep.tile([P, F], U8, name="pls", align_bytes=64)
-        out1 = out_1.rearrange("g p m t -> g p (m t)")
+        def encode_fx(c):
+            nc.vector.quantize_mx(
+                out=fx_code[c][:].rearrange("p g o -> p (g o)").bitcast(FP8X4),
+                scales=fx_scale[c][:].rearrange("p g o -> p (g o)"),
+                in_=made["f", ("x", c)][:].rearrange("p o j -> p (o j)"),
+            )
 
-        def emit(eng, out, in_):
-            if eng == "S":
+
+        plane_code = []
+        for h in range(2):
+            code = keep.tile([P, SIZE], U32, name=f"plane_code{h}", align_bytes=64)
+            plane_code.append(code)
+        plane_scale = keep.tile([P, SIZE], U8, name="plane_scale", align_bytes=64)
+        plane_words = out_1.rearrange("g p m t -> g p (m t)")
+
+        def fx_tile(tile, g):
+            c, first = tile // 2, P * (tile % 2)
+            return fx_code[c][:, g, first : first + P].bitcast(FP8X4), fx_scale[c][:, g, first : first + P]
+
+        def divide(engine, out, in_):
+            if engine == "S":
                 nc.scalar.activation(out=out, in_=in_, func=ACT.Copy, scale=INV_DIV)
             else:
                 nc.vector.tensor_scalar(out=out, in0=in_, scalar1=INV_DIV, scalar2=None, op0=ALU.mult)
 
-        def r_mm(it, h):
-            bank = psum.tile([P, 512], F32, name="bk", tag="bk", bufs=BK)
+        def cross(tile, h):
+            bank = turn_bank()
             for g in range(2):
-                a, a_s = fx(g, 128 * it, 128)
+                code, scale = fx_tile(tile, g)
                 nc.tensor.matmul_mx(
-                    out=bank[:], lhsT=a.bitcast(FP8X4), lhsT_scale=a_s,
-                    rhs=fq["y", h, g][:].rearrange("p c a -> p (c a)").bitcast(FP8X4),
-                    rhs_scale=fs["y", h, g][:].rearrange("p c a -> p (c a)"),
-                    start=(g == 0), stop=(g == 1),
+                    out=bank[:].rearrange("p t a -> p (t a)"),
+                    lhsT=code,
+                    lhsT_scale=scale,
+                    rhs=fy_code[h, g][:].rearrange("p t a -> p (t a)").bitcast(FP8X4),
+                    rhs_scale=fy_scale[h, g][:].rearrange("p t a -> p (t a)"),
+                    start=(g == 0),
+                    stop=(g == 1),
                 )
-            st["r", it, h] = bank
+            made["cross", tile, h] = bank
 
-        def r_out(it, h, eng):
-            ro = work.tile([P, 512], F32, name="ro", tag="ro", bufs=6, align_bytes=64)
-            emit(eng, ro[:].rearrange("p (a c) -> p a c", c=4), st["r", it, h][:].rearrange("p (c a) -> p a c", c=4))
-            nc.sync.dma_start(out=out_0[128 * it : 128 * it + 128, 512 * h : 512 * h + 512], in_=ro[:])
+        def store_cross(tile, h, engine):
+            r = work.tile([P, 512], F32, name="r", tag="r", bufs=6, align_bytes=64)
+            divide(engine, r[:].rearrange("p (a t) -> p a t", t=4), made["cross", tile, h][:].rearrange("p t a -> p a t"))
+            nc.sync.dma_start(out=out_0[P * tile : P * tile + P, 512 * h : 512 * h + 512], in_=r[:])
 
-        def t_mm(h, ic):
-            bank = psum.tile([P, 4, P], F32, name="bk", tag="bk", bufs=BK)
+        def cross_t(h, tile):
+            bank = turn_bank()
             for t in range(4):
                 for g in range(2):
-                    m, m_s = fx(g, 128 * ic, 128)
+                    code, scale = fx_tile(tile, g)
                     nc.tensor.matmul_mx(
                         out=bank[:, t, :],
-                        lhsT=fq["y", h, g][:, t, :].bitcast(FP8X4), lhsT_scale=fs["y", h, g][:, t, :],
-                        rhs=m.bitcast(FP8X4), rhs_scale=m_s,
-                        start=(g == 0), stop=(g == 1),
+                        lhsT=fy_code[h, g][:, t, :].bitcast(FP8X4),
+                        lhsT_scale=fy_scale[h, g][:, t, :],
+                        rhs=code,
+                        rhs_scale=scale,
+                        start=(g == 0),
+                        stop=(g == 1),
                     )
-            st["t", h, ic] = bank
+            made["cross_t", h, tile] = bank
 
-        def t_out(h, ic, eng):
-            if ("rt", h, ic // 2) not in st:
-                st["rt", h, ic // 2] = work.tile([P, 256, 4], BF16, name="rt", tag="rt", bufs=4, align_bytes=64)
-            rt = st["rt", h, ic // 2]
-            o = 128 * (ic % 2)
-            emit(eng, rt[:, o : o + 128, :], st["t", h, ic][:].rearrange("p t i -> p i t"))
+        def lift_cross_t(h, tile, engine):
+            s = work_tile("s", (h, tile // 2), [P, 256, 4], BF16, 4)
+            first = P * (tile % 2)
+            divide(engine, s[:, first : first + P, :], made["cross_t", h, tile][:].rearrange("p t i -> p i t"))
 
-        def t_quant(h, c):
+        def store_plane(h, c):
             cols = slice(256 * c, 256 * c + 256)
             nc.vector.quantize_mx(
-                out=pl_q[h][:, cols].bitcast(FP8X4),
-                scales=pl_s[4 * h : P, cols],
-                in_=st["rt", h, c][:].rearrange("p i t -> p (i t)"),
+                out=plane_code[h][:, cols].bitcast(FP8X4),
+                scales=plane_scale[4 * h : P, cols],
+                in_=made["s", (h, c)][:].rearrange("p i t -> p (i t)"),
             )
             nc.sync.dma_start(
-                out=out1[h][:, 1024 * c : 1024 * c + 1024].bitcast(I32), in_=pl_q[h][:, cols].bitcast(I32)
+                out=plane_words[h][:, 1024 * c : 1024 * c + 1024].bitcast(I32),
+                in_=plane_code[h][:, cols].bitcast(I32),
             )
 
-        def store_scales(i0, n):
+        def store_scales(part):
+            cols = slice(512 * part, 512 * part + 512)
             for quad in range(4):
                 nc.sync.dma_start(
-                    out=out_2[:, 4 * quad : 4 * quad + 4, i0 : i0 + n].bitcast(I32),
-                    in_=pl_s[32 * quad : 32 * quad + 8, i0 : i0 + n].bitcast(I32),
+                    out=out_2[:, 4 * quad : 4 * quad + 4, cols].bitcast(I32),
+                    in_=plane_scale[32 * quad : 32 * quad + 8, cols].bitcast(I32),
                 )
 
-        for n in range(WARM):
-            bank = psum.tile([P, 4, P], F32, name="bk", tag="bk", bufs=BK)
-            for m in range(4):
-                nc.tensor.transpose(bank[:, m, :], ident[:], ident[:])
-        ops = []
 
-        def at(t, f, *args):
-            ops.append((t, len(ops), f, args))
-
-        for i, f in enumerate((bias_turn, bias_nat, bias_flat, bias_flat_turn, bias_cols)):
-            at(BIAS_AT[i], f)
-        for n in range(16):
-            key = GROUPS[n // 4]
-            at(TURN_AT[n], turn, key, n % 4)
-            at(COPY_AT[n], turn_copy, key, n % 4, COPY_BY[n])
-            if n < 2:
-                at(COPY_AT[n] + TURN_QUANT, turn_quant, key, n, 1)
-            elif n % 2 == 1:
-                at(max(COPY_AT[n - 1], COPY_AT[n]) + TURN_QUANT, turn_quant, key, n % 4 - 1, 2)
-        for u in range(8):
-            t, v, w = MM_AT[u], BIAS_START[u], WEIGH_AT[u]
-            if (u, 0) in TURNED:
-                for k in range(4):
-                    g, ft = divmod(k, 2)
-                    at(t[k], zmm, u, g, ft)
-                    at(t[k] + Z_TANH, ztanh, u, g, ft)
-                    at(t[k] + Z_TURN, zturn, u, g, ft)
-                    at(v[k], zweigh, u, g, ft)
-                at(w, quant, u)
-            else:
-                for k in range(4):
-                    at(t[k], mm, u, k)
-                    at(v[k], bias, u, k)
-                for half in range(2):
-                    at(v[2 * half + 1] + TANH_LAG, tanh, u, half)
-                if UNITS[u][0] == "c":
-                    for half in range(2):
-                        at(w + WEIGH_STEP * half, weigh, u, half)
-                    at(w + WEIGH_STEP + QUANT_LAG, quant, u)
-                elif u in SOFF:
-                    for j in range(4):
-                        at(v[2 * (j // 2) + 1] + TANH_LAG + SW_LAG + 0.4 * (j % 2), sw, u, j)
-                    at(w, il, u)
-                    at(w + QUANT_LAG, quant, u)
-                else:
-                    at(w, weigh, u, 0)
-                    at(w + QUANT_LAG, quant, u)
-        n = 0
-        for h, chunks, start, step in BLOCKS:
-            t = start
-            for c in chunks:
-                for it in (2 * c, 2 * c + 1):
-                    for f, g, a, e in ((r_mm, r_out, it, h), (t_mm, t_out, h, it)):
-                        at(t, f, a, e)
-                        at(t + OUT_LAG[n], g, a, e, OUT_BY[n])
-                        t += step
-                        n += 1
-                at(t + PLANE_LAG, t_quant, h, c)
-        done = [o[0] for o in ops if o[1] >= 0 and o[2] == t_quant and o[3][1] < 2]
-        at(max(done) + 0.01, store_scales, 0, 512)
-        at(1000.0, store_scales, 512, 512)
-        for o in sorted(ops, key=lambda o: o[:2]):
-            o[2](*o[3])
+        steps = {
+            "turn": turn, "lift": lift, "encode_y": encode_y, "encode_x": encode_x,
+            "spread_bias": spread_bias, "lift_bias": lift_bias, "widen_bias": widen_bias,
+            "turn_bias": turn_bias, "lift_bias_column": lift_bias_column,
+            "dot_y": dot_y, "add_y": add_y, "tanh_y": tanh_y, "weigh_y": weigh_y,
+            "scale_y": scale_y, "weave_y": weave_y, "encode_fy": encode_fy,
+            "dot_x": dot_x, "add_x": add_x, "tanh_x": tanh_x, "weigh_x": weigh_x,
+            "dot_obs": dot_obs, "tanh_obs": tanh_obs, "turn_obs": turn_obs, "weigh_obs": weigh_obs,
+            "encode_fx": encode_fx,
+            "cross": cross, "store_cross": store_cross, "cross_t": cross_t, "lift_cross_t": lift_cross_t,
+            "store_plane": store_plane, "store_scales": store_scales,
+        }
+        for step in SCORE.split():
+            parts = step.split(".")
+            steps[parts[0]](*[int(a) if a in "01234567" else a for a in parts[1:]])

from contextlib import ExitStack

import concourse.mybir as mybir
from concourse.masks import make_identity

SIZE = 1024
P = 128
FLOPS = 3 * 2 * SIZE * SIZE * SIZE
INV_DIV = 1.0 / 32.0

F32 = mybir.dt.float32
BF16 = mybir.dt.bfloat16
U32 = mybir.dt.uint32
I32 = mybir.dt.int32
U8 = mybir.dt.uint8
FP8X4 = mybir.dt.float8_e4m3fn_x4
ACT = mybir.ActivationFunctionType
ALU = mybir.AluOpType

SUM_BANKS = 4
TURN_BANKS = 4

SCORE = """
turn.y.0.0 turn.y.0.1 lift.y.0.0.S spread_bias encode_y.0.0.1 lift_bias.S lift.y.0.1.V dot_y.0.0.0 add_y.0.0.0
turn.y.0.3 encode_y.0.1.1 turn.y.0.2 lift.y.0.3.V dot_y.0.0.1 lift.y.0.2.S turn.y.1.0 widen_bias add_y.0.0.1
turn.y.1.1 encode_y.0.2.2 lift.y.1.0.S turn.y.1.2 lift.y.1.1.S dot_y.0.0.2 lift.y.1.2.V tanh_y.0.0.0 dot_y.0.0.3
encode_y.1.0.2 turn.y.1.3 add_y.0.0.3 turn.x.0.0 add_y.0.0.2 lift.y.1.3.S dot_y.0.1.0 scale_y.0.0.0 encode_y.1.2.2
dot_y.0.1.1 tanh_y.0.0.1 add_y.0.1.0 dot_y.0.1.2 add_y.0.1.1 dot_y.0.1.3 scale_y.0.0.2 add_y.0.1.2 dot_y.1.0.3
scale_y.0.0.3 add_y.0.1.3 dot_y.1.0.2 scale_y.0.0.1 add_y.1.0.3 turn.x.0.1 lift.x.0.0.S weave_y.0.0 turn.x.0.3
lift.x.0.1.S turn.x.1.2 tanh_y.0.1.1 turn.x.0.2 encode_x.0.0 dot_y.1.0.0 add_y.1.0.2 lift.x.1.2.S dot_y.1.1.2
encode_fy.0.0 lift.x.0.2.S dot_y.1.1.0 add_y.1.0.0 lift.x.0.3.S dot_y.1.1.3 add_y.1.1.0 tanh_y.0.1.0 dot_y.1.0.1
add_y.1.1.3 turn.x.1.3 scale_y.0.1.3 encode_x.0.2 dot_y.1.1.1 lift.x.1.3.S add_y.1.0.1 turn_bias scale_y.0.1.0
encode_x.1.2 dot_x.2.0.0 scale_y.0.1.1 add_y.1.1.1 turn.x.1.0 scale_y.0.1.2 add_y.1.1.2 turn.x.1.1 lift.x.1.0.S
weave_y.0.1 dot_obs.1.0.1 lift_bias_column lift.x.1.1.S dot_obs.1.0.0 tanh_obs.1.0.1 dot_obs.0.0.0 encode_x.1.0
tanh_obs.1.0.0 dot_obs.0.0.1 add_x.2.0.0 tanh_y.1.0.1 turn_obs.1.0.0 encode_fy.0.1 dot_x.2.0.1 weigh_obs.1.0.0
tanh_y.1.0.0 turn_obs.1.0.1 add_x.2.0.1 dot_obs.1.1.0 weigh_obs.1.0.1 tanh_obs.0.0.0 dot_obs.1.1.1 weigh_y.1.0
tanh_obs.1.1.0 dot_obs.0.1.0 tanh_obs.1.1.1 turn_obs.1.1.0 turn_obs.0.0.0 tanh_obs.0.1.0 dot_obs.0.1.1 tanh_obs.0.0.1
weigh_obs.0.0.0 dot_x.3.0.0 tanh_y.1.1.1 turn_obs.1.1.1 weigh_obs.1.1.0 turn_obs.0.0.1 weigh_obs.1.1.1 dot_x.2.1.0
tanh_obs.0.1.1 weigh_obs.0.0.1 turn_obs.0.1.0 tanh_x.2.0 encode_fx.1 turn_obs.0.1.1 dot_x.2.1.1 weigh_obs.0.1.1
tanh_y.1.1.0 cross_t.0.2 weigh_obs.0.1.0 cross.3.0 add_x.2.1.1 lift_cross_t.0.2.S cross_t.0.3 encode_fx.0
store_cross.3.0.S dot_x.3.0.1 add_x.2.1.0 lift_cross_t.0.3.S cross.1.0 weigh_y.1.1 tanh_x.2.1 cross_t.0.1 cross_t.0.0
lift_cross_t.0.1.S cross.2.0 lift_cross_t.0.0.S cross.0.0 encode_fy.1.0 store_cross.2.0.S dot_x.3.1.1 encode_fy.1.1
store_cross.0.0.S add_x.3.0.1 cross.2.1 store_cross.1.0.S add_x.3.0.0 cross.3.1 store_cross.2.1.S weigh_x.2.1
cross.0.1 tanh_x.3.0 cross_t.1.0 weigh_x.2.0 dot_x.3.1.0 store_cross.0.1.S cross_t.1.2 lift_cross_t.1.0.S add_x.3.1.0
cross_t.1.1 lift_cross_t.1.2.S encode_fx.2 cross.1.1 store_cross.3.1.S weigh_x.3.0 cross_t.1.3 lift_cross_t.1.1.S
cross.4.0 store_cross.1.1.S add_x.3.1.1 cross_t.0.4 store_cross.4.0.S lift_cross_t.1.3.V cross.5.0 tanh_x.3.1
store_plane.1.0 cross_t.0.5 store_cross.5.0.V cross.4.1 lift_cross_t.0.5.S weigh_x.3.1 cross_t.1.5 lift_cross_t.0.4.S
cross.5.1 store_cross.4.1.S encode_fx.3 cross_t.1.4 store_cross.5.1.S store_plane.0.0 cross_t.1.6 store_plane.1.1
lift_cross_t.1.5.S cross.6.0 lift_cross_t.1.6.V lift_cross_t.1.4.S cross.6.1 store_plane.0.2 store_cross.6.0.S
store_plane.0.1 store_scales.0 cross_t.0.7 store_plane.1.2 store_cross.6.1.S cross_t.1.7 lift_cross_t.0.7.S cross.7.1
cross.7.0 store_cross.7.1.V cross_t.0.6 store_cross.7.0.S lift_cross_t.1.7.V lift_cross_t.0.6.S store_plane.1.3
store_plane.0.3 store_scales.1
"""


def tile_extendeddmdkoopmancrossmoment_x2_kernel(
    tc, x, y, w_words, w_scales, b, p, q, out_0, out_1, out_2
):
    nc = tc.nc
    with ExitStack() as ctx:
        keep = ctx.enter_context(tc.tile_pool(name="keep", bufs=1))
        work = ctx.enter_context(tc.tile_pool(name="work", bufs=3))
        psum = ctx.enter_context(tc.psum_pool(name="psum", bufs=1))
        ctx.enter_context(tc.manual_schedule())

        made = {}


        ident = keep.tile([P, P], F32, name="ident", align_bytes=64)
        make_identity(nc, ident[:])

        w_scale = keep.tile([P, SIZE], U8, name="w_scale", align_bytes=64)
        nc.vector.memset(w_scale[:].bitcast(I32), 0)
        zero = keep.tile([P, 1], F32, name="zero")
        nc.vector.memset(zero[:], 0.0)

        b_rows = keep.tile([P, 8], BF16, name="b_rows", align_bytes=64)
        nc.scalar.dma_start(out=b_rows[:], in_=b.rearrange("(n w) -> n w", w=8))
        for quad in range(4):
            nc.scalar.dma_start(
                out=w_scale[32 * quad : 32 * quad + 8, :].bitcast(I32),
                in_=w_scales[:, 4 * quad : 4 * quad + 4, :].bitcast(I32),
            )
        tanh_warm_up = keep.tile([P, 1], F32, name="tanh_warm_up")
        nc.scalar.activation(out=tanh_warm_up[:], in_=zero[:], func=ACT.Tanh)

        row_words = {}

        def load_rows(op, source, g, j, n):
            rows = keep.tile([P, n, SIZE], BF16, name=f"rows_{op}{g}{j}", align_bytes=64)
            nc.sync.dma_start(
                out=rows[:], in_=source.rearrange("(g p j) d -> g p j d", g=2, j=4)[g, :, j : j + n, :]
            )
            for k in range(n):
                row_words[op, g, j + k] = rows[:, k, :].bitcast(F32)

        w_code = keep.tile([P, 2, SIZE], U32, name="w_code", align_bytes=64)
        w_source = w_words.rearrange("c p n t -> p c (n t)")

        def load_w(h):
            nc.sync.dma_start(
                out=w_code[:, :, 512 * h : 512 * h + 512].bitcast(I32),
                in_=w_source[:, :, 2048 * h : 2048 * h + 2048].bitcast(I32),
            )

        weight = {}
        weight_f32 = {}

        def load_weights(op, source):
            weight[op] = keep.tile([P, 2, 4], BF16, name=f"weight_{op}", align_bytes=64)
            nc.sync.dma_start(out=weight[op][:], in_=source.rearrange("(g p j) -> p g j", g=2, j=4))
            weight_f32[op] = keep.tile([P, 2, 4], F32, name=f"weight_f32_{op}", align_bytes=64)
            nc.gpsimd.tensor_copy(out=weight_f32[op][:], in_=weight[op][:])

        load_rows("y", y, 0, 0, 1)
        load_rows("y", y, 0, 1, 1)
        load_w(0)
        load_rows("y", y, 0, 2, 2)
        load_rows("y", y, 1, 0, 2)
        load_rows("y", y, 1, 2, 2)
        load_weights("y", q)
        load_weights("x", p)
        load_rows("x", x, 0, 0, 4)
        load_rows("x", x, 1, 0, 4)
        load_w(1)

        def turn_bank():
            bank = psum.tile([P, 4, P], F32, name="turn_bank", tag="turn_bank", bufs=TURN_BANKS)
            return bank

        def sum_bank():
            bank = psum.tile([P, 512], F32, name="sum_bank", tag="sum_bank", bufs=SUM_BANKS)
            return bank

        for n in range(3):
            bank = turn_bank()
            for m in range(4):
                nc.tensor.transpose(bank[:, m, :], ident[:], ident[:])


        row_dims = {"y": [P, 4, 2, P], "x": [P, 2, 4, P]}
        row_code = {}
        row_scale = {}
        for op in ("y", "x"):
            for g in range(2):
                row_code[op, g] = keep.tile(row_dims[op], U32, name=f"row_code_{op}{g}", align_bytes=64)
                row_scale[op, g] = keep.tile(row_dims[op], U8, name=f"row_scale_{op}{g}", align_bytes=64)

        def stationary_rows(op, g, j, c):
            if op == "y":
                return row_code[op, g][:, j, c, :].bitcast(FP8X4), row_scale[op, g][:, j, c, :]
            return row_code[op, g][:, c, j, :].bitcast(FP8X4), row_scale[op, g][:, c, j, :]

        def copy(engine, out, in_):
            if engine == "S":
                nc.scalar.copy(out=out, in_=in_)
            else:
                nc.vector.tensor_copy(out=out, in_=in_)

        def turn(op, g, j):
            bank = turn_bank()
            words = row_words[op, g, j]
            for c in range(2):
                for e in range(2):
                    nc.tensor.transpose(bank[:, 2 * c + e, :], words[:, 256 * c + e : 256 * (c + 1) : 2], ident[:])
            made["turn", op, g, j] = bank

        def lift(op, g, j, engine):
            if ("lift", op, g, j // 2) not in made:
                pair_dims = [P, 2, 2, P, 2]
                made["lift", op, g, j // 2] = work.tile(pair_dims, F32, name="pair", tag="pair", align_bytes=64)
            pair = made["lift", op, g, j // 2]
            out = pair[:, j % 2] if op == "y" else pair[:, :, j % 2]
            copy(engine, out, made["turn", op, g, j][:].rearrange("p (c e) r -> p c r e", e=2))

        def encode_y(g, j, n):
            pair = made["lift", "y", g, j // 2]
            nc.vector.quantize_mx(
                out=row_code["y", g][:, j : j + n].rearrange("p j c r -> p (j c r)").bitcast(FP8X4),
                scales=row_scale["y", g][:, j : j + n].rearrange("p j c r -> p (j c r)"),
                in_=pair[:, j % 2 : j % 2 + n].rearrange("p j c r e -> p (j c r e)").bitcast(BF16),
            )

        def encode_x(g, j):
            for c in range(2):
                nc.vector.quantize_mx(
                    out=row_code["x", g][:, c, j : j + 2].rearrange("p j r -> p (j r)").bitcast(FP8X4),
                    scales=row_scale["x", g][:, c, j : j + 2].rearrange("p j r -> p (j r)"),
                    in_=made["lift", "x", g, j // 2][:, c].rearrange("p j r e -> p (j r e)").bitcast(BF16),
                )


        bias_words = keep.tile([P, P, 4], F32, name="bias_words", align_bytes=64)
        bias_row = bias_words[:].rearrange("p n m -> p (n m)").bitcast(BF16)
        bias_f32 = keep.tile([P, 4, P], F32, name="bias_f32", align_bytes=64)
        bias_column = keep.tile([P, 4], F32, name="bias_column", align_bytes=64)

        def spread_bias():
            made["spread_bias"] = turn_bank()
            words = b_rows[:].bitcast(F32)
            for m in range(4):
                nc.tensor.transpose(made["spread_bias"][:, m, :], words[:, m : m + 1].to_broadcast([P, P]), ident[:])

        def lift_bias(engine):
            copy(engine, bias_words[:], made["spread_bias"][:].rearrange("p m n -> p n m"))

        def widen_bias():
            nc.scalar.copy(out=bias_f32[:].rearrange("p m n -> p (m n)"), in_=bias_row[:, 0:512])

        def turn_bias():
            made["turn_bias"] = turn_bank()
            for m in range(4):
                nc.tensor.transpose(made["turn_bias"][:, m, :], bias_f32[:, m, :], ident[:])

        def lift_bias_column():
            nc.scalar.copy(out=bias_column[:], in_=made["turn_bias"][:, :, 0])


        fy_code = {}
        fy_scale = {}
        for h in range(2):
            for g in range(2):
                fy_code[h, g] = keep.tile([P, 4, P], U32, name=f"fy_code{h}{g}", align_bytes=64)
                fy_scale[h, g] = keep.tile([P, 4, P], U8, name=f"fy_scale{h}{g}", align_bytes=64)
        fx_code = []
        fx_scale = []
        for c in range(4):
            code = keep.tile([P, 2, 256], U32, name=f"fx_code{c}", align_bytes=64)
            scale = keep.tile([P, 2, 256], U8, name=f"fx_scale{c}", align_bytes=64)
            fx_code.append(code)
            fx_scale.append(scale)

        def work_tile(name, key, dims, dtype, bufs):
            if (name, key) not in made:
                made[name, key] = work.tile(dims, dtype, name=name, tag=name, bufs=bufs, align_bytes=64)
            return made[name, key]

        def project(op, g, j, col, n, out):
            for c in range(2):
                code, scale = stationary_rows(op, g, j, c)
                nc.tensor.matmul_mx(
                    out=out,
                    lhsT=code,
                    lhsT_scale=scale,
                    rhs=w_code[:, c, col : col + n].bitcast(FP8X4),
                    rhs_scale=w_scale[4 * c : P, col : col + n],
                    start=(c == 0),
                    stop=(c == 1),
                )


        def dot_y(h, g, j):
            bank = sum_bank()
            project("y", g, j, 512 * h, 512, bank[:])
            made["dot_y", h, g, j] = bank

        def add_y(h, g, j):
            z = work_tile("z", ("y", h, g), [P, 2048], F32, 3)
            nc.vector.tensor_tensor(
                out=z[:, 512 * j : 512 * j + 512].rearrange("p (t a) -> p t a", t=4),
                in0=made["dot_y", h, g, j][:].rearrange("p (a t) -> p t a", t=4),
                in1=bias_row[:, 512 * h : 512 * h + 512].rearrange("p (a t) -> p t a", t=4),
                op=ALU.add,
            )

        def tanh(key, part):
            span = slice(1024 * part, 1024 * part + 1024)
            th = work_tile("th", key, [P, 2048], F32, 3)
            nc.scalar.activation(out=th[:, span], in_=made["z", key][:, span], func=ACT.Tanh)

        def tanh_y(h, g, part):
            tanh(("y", h, g), part)

        def weave(f, th, weights, n):
            nc.vector.tensor_tensor(
                out=f.rearrange("p (o i) j -> p o j i", i=4),
                in0=th.rearrange("p j (o i) -> p o j i", i=4),
                in1=weights.unsqueeze(1).unsqueeze(3).to_broadcast([P, n // 4, 4, 4]),
                op=ALU.mult,
            )

        def weigh_y(h, g):
            f = work_tile("f", ("y", h, g), [P, 512, 4], BF16, 3)
            weave(f[:], made["th", ("y", h, g)][:].rearrange("p (j o) -> p j o", j=4), weight["y"][:, g, :], 512)


        def scale_y(h, g, j):
            v = work_tile("v", ("y", h, g), [P, 4, 512], BF16, 2)
            nc.scalar.activation(
                out=v[:, j, :],
                in_=made["th", ("y", h, g)][:, 512 * j : 512 * j + 512],
                func=ACT.Copy,
                scale=weight_f32["y"][:, g, j : j + 1],
            )

        def weave_y(h, g):
            f = work_tile("f", ("y", h, g), [P, 512, 4], BF16, 3)
            nc.vector.tensor_copy(
                out=f[:].rearrange("p (o i) j -> p o j i", i=4),
                in_=made["v", ("y", h, g)][:].rearrange("p j (o i) -> p o j i", i=4),
            )

        def encode_fy(h, g):
            nc.vector.quantize_mx(
                out=fy_code[h, g][:].rearrange("p t a -> p (t a)").bitcast(FP8X4),
                scales=fy_scale[h, g][:].rearrange("p t a -> p (t a)"),
                in_=made["f", ("y", h, g)][:].rearrange("p o j -> p (o j)"),
            )


        def dot_x(c, g, i):
            bank = sum_bank()
            for k in range(2):
                project("x", g, 2 * i + k, 256 * c, 256, bank[:, 256 * k : 256 * k + 256])
            made["dot_x", c, g, i] = bank

        def add_x(c, g, i):
            z = work_tile("z", ("x", c), [P, 2048], F32, 3)
            first = 1024 * g + 512 * i
            nc.vector.tensor_tensor(
                out=z[:, first : first + 512].rearrange("p (k o) -> p k o", k=2),
                in0=made["dot_x", c, g, i][:].rearrange("p (k o) -> p k o", k=2),
                in1=bias_row[:, 256 * c : 256 * c + 256].unsqueeze(1).to_broadcast([P, 2, 256]),
                op=ALU.add,
            )

        def tanh_x(c, g):
            tanh(("x", c), g)

        def weigh_x(c, g):
            f = work_tile("f", ("x", c), [P, 512, 4], BF16, 3)
            th = made["th", ("x", c)][:, 1024 * g : 1024 * g + 1024].rearrange("p (j o) -> p j o", j=4)
            weave(f[:, 256 * g : 256 * g + 256, :], th, weight["x"][:, g, :], 256)


        def dot_obs(c, g, i):
            col = 256 * c + 128 * i
            bank = sum_bank()
            for k in range(2):
                nc.tensor.matmul_mx(
                    out=bank[:],
                    lhsT=w_code[:, k, col : col + P].bitcast(FP8X4),
                    lhsT_scale=w_scale[4 * k : P, col : col + P],
                    rhs=row_code["x", g][:, k].rearrange("p j r -> p (j r)").bitcast(FP8X4),
                    rhs_scale=row_scale["x", g][:, k].rearrange("p j r -> p (j r)"),
                    start=(k == 0),
                    stop=(k == 1),
                )
            made["dot_obs", c, g, i] = bank

        def tanh_obs(c, g, i):
            t = work_tile("t", (c, g, i), [P, 4, P], F32, 3)
            nc.scalar.activation(
                out=t[:].rearrange("p j r -> p (j r)"),
                in_=made["dot_obs", c, g, i][:],
                func=ACT.Tanh,
                bias=bias_column[:, 2 * c + i : 2 * c + i + 1],
            )

        def turn_obs(c, g, i):
            bank = turn_bank()
            for j in range(4):
                nc.tensor.transpose(bank[:, j, :], made["t", (c, g, i)][:, j, :], ident[:])
            made["turn_obs", c, g, i] = bank

        def weigh_obs(c, g, i):
            f = work_tile("f", ("x", c), [P, 512, 4], BF16, 3)
            first = 256 * g + 128 * i
            nc.vector.tensor_tensor(
                out=f[:, first : first + P, :],
                in0=made["turn_obs", c, g, i][:].rearrange("p j o -> p o j"),
                in1=weight["x"][:, g, :].unsqueeze(1).to_broadcast([P, P, 4]),
                op=ALU.mult,
            )

        def encode_fx(c):
            nc.vector.quantize_mx(
                out=fx_code[c][:].rearrange("p g o -> p (g o)").bitcast(FP8X4),
                scales=fx_scale[c][:].rearrange("p g o -> p (g o)"),
                in_=made["f", ("x", c)][:].rearrange("p o j -> p (o j)"),
            )


        plane_code = []
        for h in range(2):
            code = keep.tile([P, SIZE], U32, name=f"plane_code{h}", align_bytes=64)
            plane_code.append(code)
        plane_scale = keep.tile([P, SIZE], U8, name="plane_scale", align_bytes=64)
        plane_words = out_1.rearrange("g p m t -> g p (m t)")

        def fx_tile(tile, g):
            c, first = tile // 2, P * (tile % 2)
            return fx_code[c][:, g, first : first + P].bitcast(FP8X4), fx_scale[c][:, g, first : first + P]

        def divide(engine, out, in_):
            if engine == "S":
                nc.scalar.activation(out=out, in_=in_, func=ACT.Copy, scale=INV_DIV)
            else:
                nc.vector.tensor_scalar(out=out, in0=in_, scalar1=INV_DIV, scalar2=None, op0=ALU.mult)

        def cross(tile, h):
            bank = turn_bank()
            for g in range(2):
                code, scale = fx_tile(tile, g)
                nc.tensor.matmul_mx(
                    out=bank[:].rearrange("p t a -> p (t a)"),
                    lhsT=code,
                    lhsT_scale=scale,
                    rhs=fy_code[h, g][:].rearrange("p t a -> p (t a)").bitcast(FP8X4),
                    rhs_scale=fy_scale[h, g][:].rearrange("p t a -> p (t a)"),
                    start=(g == 0),
                    stop=(g == 1),
                )
            made["cross", tile, h] = bank

        def store_cross(tile, h, engine):
            r = work.tile([P, 512], F32, name="r", tag="r", bufs=6, align_bytes=64)
            divide(engine, r[:].rearrange("p (a t) -> p a t", t=4), made["cross", tile, h][:].rearrange("p t a -> p a t"))
            nc.sync.dma_start(out=out_0[P * tile : P * tile + P, 512 * h : 512 * h + 512], in_=r[:])

        def cross_t(h, tile):
            bank = turn_bank()
            for t in range(4):
                for g in range(2):
                    code, scale = fx_tile(tile, g)
                    nc.tensor.matmul_mx(
                        out=bank[:, t, :],
                        lhsT=fy_code[h, g][:, t, :].bitcast(FP8X4),
                        lhsT_scale=fy_scale[h, g][:, t, :],
                        rhs=code,
                        rhs_scale=scale,
                        start=(g == 0),
                        stop=(g == 1),
                    )
            made["cross_t", h, tile] = bank

        def lift_cross_t(h, tile, engine):
            s = work_tile("s", (h, tile // 2), [P, 256, 4], BF16, 4)
            first = P * (tile % 2)
            divide(engine, s[:, first : first + P, :], made["cross_t", h, tile][:].rearrange("p t i -> p i t"))

        def store_plane(h, c):
            cols = slice(256 * c, 256 * c + 256)
            nc.vector.quantize_mx(
                out=plane_code[h][:, cols].bitcast(FP8X4),
                scales=plane_scale[4 * h : P, cols],
                in_=made["s", (h, c)][:].rearrange("p i t -> p (i t)"),
            )
            nc.sync.dma_start(
                out=plane_words[h][:, 1024 * c : 1024 * c + 1024].bitcast(I32),
                in_=plane_code[h][:, cols].bitcast(I32),
            )

        def store_scales(part):
            cols = slice(512 * part, 512 * part + 512)
            for quad in range(4):
                nc.sync.dma_start(
                    out=out_2[:, 4 * quad : 4 * quad + 4, cols].bitcast(I32),
                    in_=plane_scale[32 * quad : 32 * quad + 8, cols].bitcast(I32),
                )


        steps = {
            "turn": turn, "lift": lift, "encode_y": encode_y, "encode_x": encode_x,
            "spread_bias": spread_bias, "lift_bias": lift_bias, "widen_bias": widen_bias,
            "turn_bias": turn_bias, "lift_bias_column": lift_bias_column,
            "dot_y": dot_y, "add_y": add_y, "tanh_y": tanh_y, "weigh_y": weigh_y,
            "scale_y": scale_y, "weave_y": weave_y, "encode_fy": encode_fy,
            "dot_x": dot_x, "add_x": add_x, "tanh_x": tanh_x, "weigh_x": weigh_x,
            "dot_obs": dot_obs, "tanh_obs": tanh_obs, "turn_obs": turn_obs, "weigh_obs": weigh_obs,
            "encode_fx": encode_fx,
            "cross": cross, "store_cross": store_cross, "cross_t": cross_t, "lift_cross_t": lift_cross_t,
            "store_plane": store_plane, "store_scales": store_scales,
        }
        for step in SCORE.split():
            parts = step.split(".")
            steps[parts[0]](*[int(a) if a in "01234567" else a for a in parts[1:]])
